import numpy as np, ml_dtypes
CORES = [36,164,52,180,100,228,116,244]
N = 8
import mx_ref
BF = ml_dtypes.bfloat16
def cols(t, e):
    v = np.concatenate([t.reshape(128, -1, 4), np.zeros((128, 1, 4), BF)], axis=1)
    return np.ascontiguousarray(v[:, e]).reshape(128, -1)
def f(rng, *shape):
    return mx_ref.flush((rng.standard_normal(shape, dtype=np.float32) * np.exp2(rng.integers(-2, 3, shape[:-1] + (1,)))).astype(BF))
def wide(rng, *shape, cols=0):
    v = rng.standard_normal(shape, dtype=np.float32) * np.exp2(rng.integers(-12, 13, shape)).astype(np.float32)
    if cols: v *= np.repeat(np.exp2(rng.integers(-cols, cols + 1, shape[:-2] + (1, shape[-1] // 4))) * (rng.random(shape[:-2] + (1, shape[-1] // 4)) > 0.0625), 4, axis=-1).astype(np.float32)
    return mx_ref.flush(v.astype(BF))
T, K, O = 256, 128, 2
def setup_inputs(rng):
    u = np.zeros((128, 512), BF); u[:, :4] = f(rng, 128, 4)
    return {"x": f(rng, N, 128, 4 * T), "u": np.stack([u] * N), "w": f(rng, N, 128, 512 * O)}
def signs(d):
    return np.where(d["u"][0][:, :4].astype(np.float32) < 0, -1, 1).astype(np.float32)
def blocks(rng, n):
    return np.repeat(rng.permutation(16) < n, 8)
def plant(rng, d, n):
    for s in range(N):
        v = d["x"][s].astype(np.float32).reshape(128, T, 4)
        k = rng.permutation(T)[:n[s]]
        v[:, k] = np.abs(v[:, k]) * signs(d)[:, None] * np.float32(8)
        d["x"][s] = v.reshape(128, -1).astype(BF)
    return d
def setup_inputs_one(rng):
    d = setup_inputs(rng); return plant(rng, d, np.where(np.arange(N) == rng.integers(0, N), K, 0))
def setup_inputs_zeros(rng):
    d = setup_inputs(rng); m = blocks(rng, 2)
    d["u"][:, ~m] = 0
    k = rng.permutation(N * T); g = np.full(N * T, -1, np.float32)
    g[k[:K // 3]] = 1; g[k[K // 3:2 * (K // 3)]] = 0
    v = np.abs(d["x"][:, m].astype(np.float32)).reshape(N, -1, T, 4)
    d["x"][:, m] = (v * signs(d)[m][:, None] * g.reshape(N, 1, T, 1)).reshape(N, -1, 4 * T).astype(BF)
    return d
def setup_inputs_few(rng):
    d = setup_inputs(rng); p = rng.permutation(N); g = p[N - N // 2:]
    d["x"][g] = (-np.abs(d["x"][g].astype(np.float32)) * np.tile(signs(d), (1, T))).astype(BF)
    n = np.zeros(N, int); n[p[:2]] = [K * 3 // 5, K - K * 3 // 5]
    return plant(rng, d, n)
def setup_inputs_ties(rng):
    d = setup_inputs(rng); b = f(rng, 128, 4 * 40); m = blocks(rng, 4)
    d["u"][:, m] = 0
    d["x"] = np.stack([cols(b, rng.permutation(np.arange(T) % 40)) for r in range(N)])
    d["x"][:, m] = f(rng, N, 32, 4 * T); return d
def setup_inputs_spread(rng):
    d = setup_inputs(rng); d["x"] = wide(rng, N, 128, 4 * T, cols=8); return d
def check_inputs(d):
    b = []
    u = d["u"].astype(np.float32)
    if (u != u[:1]).any(): b.append("u_same")
    if (u[:, :, 4:] != 0).any(): b.append("u_zero")
    return b
def reference(x, u, w):
    s = np.stack([mx_ref.matmul(mx_ref.quantize(u[r]), mx_ref.quantize(x[r]))[0] for r in range(N)]).reshape(-1) + np.float32(0.0)
    best = np.lexsort((np.arange(N * T), -s))[:K]
    V = mx_ref.quantize(cols(np.concatenate(list(x), axis=1), best))
    y = np.zeros((N, 128, O * K), np.float32)
    for r in range(N):
        for o in range(O): y[r][:, K * o:K * o + K] = mx_ref.matmul(mx_ref.quantize(np.ascontiguousarray(w[r][:, 512 * o:512 * o + 512])), V)
    who = np.stack([best // T, best % T]).astype(np.float32)
    return {"y": y, "id": np.stack([who] * N)}

@@ -1,0 +1,396 @@
+from concourse.bass import DstId, RemoteDMATransfer
+from concourse.mybir import dt, AluOpType, ActivationFunctionType
+
+N, T_COLS, K, O = 8, 256, 128, 2
+BF, F32, U16, I32, CODE, U8 = "bfloat16", "float32", "uint16", "int32", "float8_e4m3fn_x4", "uint8"
+OTH = 64 * (N - 1)
+ZC = 16
+
+
+def _sbuf(cols, dtype, names):
+    return {n: ("sbuf", [128, cols], dtype) for n in names.split()}
+
+
+SCRATCH = {}
+SCRATCH.update(_sbuf(512, BF, "UT"))
+SCRATCH.update(_sbuf(1024 + 4 * ZC, BF, "XT"))
+SCRATCH.update(_sbuf(1024, BF, "WT"))
+SCRATCH.update(_sbuf(128, CODE, "UQ0 UQ V4Q L4Q"))
+SCRATCH.update(_sbuf(128, U8, "US0 US V4S L4S"))
+SCRATCH.update(_sbuf(256, CODE, "WQ W1Q"))
+SCRATCH.update(_sbuf(256, U8, "WS W1S"))
+SCRATCH.update(_sbuf(256 + ZC, CODE, "XQ ZQ"))
+SCRATCH.update(_sbuf(256 + ZC, U8, "XS ZS"))
+SCRATCH.update(_sbuf(8, U16, "UOFF NN LOF LUG LC LID LIA"))
+SCRATCH.update(_sbuf(2, U16, "ZOFF"))
+SCRATCH.update(_sbuf(16, U16, "LU"))
+SCRATCH.update(_sbuf(32, U16, "LV4"))
+SCRATCH.update(_sbuf(4 * (N - 1), U16, "GOFF"))
+SCRATCH.update(_sbuf(4 * (N - 1), BF, "GO"))
+SCRATCH.update(_sbuf(1, I32, "PIDX MI MJ"))
+SCRATCH.update(_sbuf(8, I32, "FO TM TC TK NI"))
+SCRATCH.update(_sbuf(16, I32, "MO SM"))
+SCRATCH.update(_sbuf(32, I32, "VI AN GN SN"))
+SCRATCH.update(_sbuf(1, F32, "MF PF MF1 SC0 SC LR PM"))
+SCRATCH.update(_sbuf(2, F32, "SCO"))
+SCRATCH.update(_sbuf(16, F32, "SCR"))
+SCRATCH.update(_sbuf(4, F32, "PG X1 P2 X2 P3 K128"))
+SCRATCH.update(_sbuf(256, BF, "JC TRI EQ LRF LH INV IDO IDA"))
+SCRATCH.update(_sbuf(128, BF, "J128 TMOD HOLD HE HB BASE ZB G GX FX FH NH CB KCB BXG GFX GH"))
+SCRATCH.update(_sbuf(1280, BF, "RTO RTA CT"))
+SCRATCH.update(_sbuf(768, BF, "CH"))
+SCRATCH.update(_sbuf(192, BF, "LS"))
+SCRATCH.update(_sbuf(64, BF, "BX"))
+SCRATCH.update(_sbuf(4 * OTH, BF, "CM"))
+SCRATCH.update(_sbuf(OTH, F32, "EX0 EX"))
+SCRATCH.update(_sbuf(128, F32, "ST SW VC VAL EH"))
+SCRATCH.update(_sbuf(256, F32, "E1 YB IDB"))
+PSUM_NAMES = ["BSF", "BS0", "BS1", "BA", "BB", "BY0", "BY1"]
+SCRATCH.update({n: ("psum", [128, 512], F32) for n in PSUM_NAMES})
+SEMAPHORES = ["v", "s", "t", "gc", "du", "dx0", "dx1", "dw0", "dw1", "dy", "did", "loc",
+              "arr1", "arr2", "arr3", "sc", "num1", "num3"]
+
+
+def rank_program(g, core, T, topo):
+    rank = T.rank_of(core)
+    if rank is None:
+        return
+    A = AluOpType
+    F = ActivationFunctionType
+    engines = {"v": g.vector, "s": g.scalar, "t": g.tensor, "g": g, "y": g.sync}
+    known = {q: {} for q in engines}
+    total = {}
+    hist = {}
+
+    def parts(r):
+        return (r[4], r[5]) if len(r) > 4 else (0, 128)
+
+    def record(reads, writes, q, sem, val, clock):
+        for rs, w in ((reads, False), (writes, True)):
+            for r in rs:
+                hist.setdefault(r[0], []).append((r[1], r[2]) + parts(r) + (w, q, sem, val, clock))
+
+    def hold(q, reads, writes):
+        need = {}
+        for rs, w in ((reads, False), (writes, True)):
+            for r in rs:
+                psum = r[0] in PSUM_NAMES
+                a, z = parts(r)
+                for lo, hi, p0, p1, hw, hq, sem, val, clock in hist.get(r[0], []):
+                    if not (psum or (lo < r[2] and r[1] < hi and p0 < z and a < p1)):
+                        continue
+                    if not (w or hw or (psum and hq != q)):
+                        continue
+                    if known[q].get(sem, 0) < val and (sem not in need or need[sem][0] < val):
+                        need[sem] = (val, clock)
+        for sem in sorted(need):
+            val, clock = need[sem]
+            if any(o != sem and need[o][1].get(sem, 0) >= val for o in need):
+                continue
+            engines[q].wait_ge(T.sem[sem], val)
+        for sem in need:
+            val, clock = need[sem]
+            for s, x in list(clock.items()) + [(sem, val)]:
+                known[q][s] = max(known[q].get(s, 0), x)
+
+    def do(q, call, writes, reads, sem=None, inc=1):
+        sem = sem or {"g": "gc"}.get(q, q)
+        hold(q, reads, writes)
+        call().then_inc(T.sem[sem], inc)
+        total[sem] = total.get(sem, 0) + inc
+        clock = dict(known[q])
+        clock[sem] = total[sem]
+        record(reads, writes, q, sem, total[sem], clock)
+
+    def ap(r):
+        if len(r) == 3:
+            return T[r[0]][:, r[1]:r[2]]
+        p, z = parts(r)
+        return T[r[0]][p:z, r[1]:r[2]:r[3]]
+
+    def words(r):
+        return ap(r).bitcast(dt.uint32)
+
+    def ts2(out, in0, s, s2, op0, op1):
+        cols = [x for x in (s, s2) if isinstance(x, tuple)]
+        a, b = [ap(x) if isinstance(x, tuple) else x for x in (s, s2)]
+        last = () if op1 is None else (op1,)
+        do("v", lambda: g.vector.tensor_scalar(ap(out), ap(in0), a, b, op0, *last), [out], [in0] + cols)
+
+    def ts(out, in0, s, op):
+        ts2(out, in0, s, None, op, None)
+
+    def tt(out, a, b, op):
+        do("v", lambda: g.vector.tensor_tensor(ap(out), ap(a), ap(b), op), [out], [a, b])
+
+    def scan(out, a, b, init, op0, op1):
+        do("v", lambda: g.vector.tensor_tensor_scan(ap(out), ap(a), ap(b), init, op0, op1), [out], [a, b])
+
+    def turn(out, a):
+        do("v", lambda: g.vector.transpose(ap(out), ap(a)), [out], [a])
+
+    def copy(out, a):
+        do("v", lambda: g.vector.tensor_copy(ap(out), ap(a)), [out], [a])
+
+    def scopy(out, a):
+        do("s", lambda: g.scalar.activation(ap(out), ap(a), F.Copy), [out], [a])
+
+    def vpick(out, win, off):
+        do("v", lambda: g.vector.tensor_copy(ap(out), ap(win).indirect(ap(off))), [out], [win, off])
+
+    def vput(win, off, src):
+        do("v", lambda: g.vector.tensor_copy(ap(win).indirect(ap(off)), ap(src)), [win], [off, src])
+
+    def spick(out, win, off):
+        do("s", lambda: g.scalar.activation(ap(out), ap(win).indirect(ap(off)), F.Copy), [out], [win, off])
+
+    def pick_columns(out, win, off):
+        do("v", lambda: g.vector.tensor_copy(words(out[0]), words(win[0]).indirect(ap(off))), [out[0]], [win[0], off])
+        spick(out[1], win[1], off)
+
+    def fill(out, x):
+        do("v", lambda: g.vector.memset(ap(out), x), [out], [])
+
+    def iota(out, pattern, base, cm):
+        do("g", lambda: g.iota(ap(out), pattern, base, cm, allow_small_or_imprecise_dtypes=True), [out], [])
+
+    def quant(q, s, t):
+        do("v", lambda: g.vector.quantize_mx(ap(q), ap(s), ap(t)), [q, s], [t])
+
+    def mm(out, wq, ws, xq, xs, start=True, stop=True):
+        do("t", lambda: g.tensor.matmul_mx(ap(out), ap(wq), ap(ws), ap(xq), ap(xs), start, stop), [out], [wq, ws, xq, xs])
+
+    def accum(buf, out):
+        do("s", lambda: g.scalar.activation(ap(buf), ap(buf), F.Identity, accum_out=ap(out)), [buf, out], [buf])
+
+    def hold16(tmp, x):
+        scan(tmp, ("HB", 0, tmp[2] - tmp[1]), x, 0.0, A.mult, A.max)
+
+    def take16(out, tmp, less):
+        ts2(out, (tmp[0], tmp[1] + 15, tmp[2], 16), ("SC", 0, 1), less, A.mult, A.subtract)
+
+    def load(q, out, src, sem):
+        do(q, lambda: engines[q].dma_start(ap(out), src), [out], [], sem, 16)
+
+    def sent(mate, rsem, copies=1):
+        n = len(topo.engines(core, T.cores[mate]))
+        total["loc"] = total.get("loc", 0) + n
+        total[rsem] = total.get(rsem, 0) + n * copies
+
+    def send(mate, out, src, rsem, codes=False):
+        dst = T.cores[mate]
+        hold("g", [src], [])
+        rid, pid = topo.addr(dst, core)
+        a, b = (ap(out).bitcast(dt.uint8), ap(src).bitcast(dt.uint8)) if codes else (ap(out), ap(src))
+        g.remote_dma(a, b, T.sem[rsem], T.sem["loc"], pid, rid, topo.mask(core, dst))
+        sent(mate, rsem)
+
+    def spread(mates, outs, src, rsem):
+        hold("g", [src], [])
+        ids = [topo.addr(T.cores[m], core) for m in mates]
+        g.remote_dma_fused([RemoteDMATransfer(
+            dst_ids=[DstId(rid=rid, pnc=pid) for rid, pid in ids], dma_engine_mask=topo.mask(core, T.cores[mates[0]]),
+            remote_sem=T.sem[rsem], src=ap(src), dsts=[ap(o) for o in outs])], local_sem=T.sem["loc"])
+        sent(mates[0], rsem, len(mates))
+
+    def arrive(regions, sem):
+        record([], regions, "-", sem, total[sem], {sem: total[sem]})
+
+    def exchange(mate, out, src, sem):
+        send(mate, out[0], src[0], sem, codes=True)
+        send(mate, out[1], src[1], sem)
+
+    def window(name, a, b):
+        return (name + "Q", a, b), (name + "S", a, b)
+
+    high = rank & 1
+
+    load("y", ("UT", 0, 8), T.u[:, 0:8], "du")
+    load("s", ("XT", 0, 512), T.x[:, 0:512], "dx0")
+    load("y", ("XT", 512, 1024), T.x[:, 512:1024], "dx1")
+
+    fill(("UT", 8, 512), 0.0)
+    fill(("XT", 1024, 1024 + 4 * ZC), 0.0)
+    fill(("UOFF", 0, 8), 0)
+    iota(("PIDX", 0, 1), [[0, 1]], 0, 1)
+    iota(("J128", 0, 128), [[1, 128]], 0, 0)
+    iota(("TMOD", 0, 128), [[0, 8], [1, 16]], 0, 0)
+    iota(("JC", 0, 256), [[32, 4], [128, 2], [1, 32]], 1, 0)
+    if rank:
+        iota(("GO", 0, 4 * rank), [[1, 2 * rank], [0, 2]], 0, 0)
+    if rank < N - 1:
+        iota(("GO", 4 * rank, 4 * (N - 1)), [[1, 2 * (N - 1 - rank)], [0, 2]], 2 * rank + 2, 0)
+    ts(("MI", 0, 1), ("PIDX", 0, 1), 15, A.bitwise_and)
+    ts(("MJ", 0, 1), ("PIDX", 0, 1), 31, A.bitwise_and)
+    copy(("PF", 0, 1), ("PIDX", 0, 1))
+    copy(("MF", 0, 1), ("MI", 0, 1))
+    copy(("PM", 0, 1), ("MJ", 0, 1))
+    for h in (0, 1):
+        ts(("TRI", 128 * h, 128 * h + 128), ("J128", 0, 128), ("PF", 0, 1), A.is_lt)
+
+    quant(("UQ0", 0, 128), ("US0", 0, 128), ("UT", 0, 512))
+    U = (("UQ", 0, 128), ("US", 0, 128))
+    pick_columns(U, (("UQ0", 0, 128), ("US0", 0, 128)), ("UOFF", 0, 8))
+    quant(("XQ", 0, 128), ("XS", 0, 128), ("XT", 0, 512))
+    quant(("XQ", 128, 256 + ZC), ("XS", 128, 256 + ZC), ("XT", 512, 1024 + 4 * ZC))
+    for h in (0, 1):
+        mm(("BY%d" % h, 0, 128), *window("X", 128 * h, 128 * h + 128), *U)
+        scopy(("SCO", h, h + 1), ("BY%d" % h, 0, 1))
+        if h == 0:
+            mm(("BS0", 0, 128), *window("X", 0, 128), *U)
+            mm(("BSF", 0, 256), *U, *window("X", 0, 256))
+    mm(("BS1", 0, 128), *window("X", 128, 256), *U)
+    others = [s for s in range(N) if s != rank]
+    spread(others, [("SCR", 2 * rank, 2 * rank + 2)] * (N - 1), ("SCO", 0, 2), "sc")
+    arrive([("SCR", 0, 16)], "sc")
+    fill(("ZB", 0, 128), 0.0)
+    ts(("MF1", 0, 1), ("MF", 0, 1), 1.0, A.add)
+    ts2(("SC0", 0, 1), ("MF", 0, 1), 15.0, 255.0 / 256.0, A.is_equal, A.mult)
+    ts(("HOLD", 0, 128), ("TMOD", 0, 128), ("MF", 0, 1), A.is_gt)
+    ts2(("HE", 0, 128), ("TMOD", 0, 128), ("MF1", 0, 1), 255.0, A.is_equal, A.mult)
+    ts(("SC", 0, 1), ("SC0", 0, 1), 1.0 / 256.0, A.add)
+
+    s0, s1 = ("BS0", 0, 1), ("BS1", 0, 1)
+    ts(("EQ", 0, 128), ("BSF", 0, 128), s0, A.is_equal)
+    ts(("EQ", 128, 256), ("BSF", 128, 256), s1, A.is_equal)
+    ts(("CH", 0, 256), ("BSF", 0, 256), s0, A.is_gt)
+    tt(("CH", 256, 512), ("EQ", 0, 256), ("TRI", 0, 256), A.mult)
+    accum(("CH", 0, 384), ("LR", 0, 1))
+    ts(("CH", 512, 640), ("BSF", 0, 128), s1, A.is_ge)
+    ts(("CH", 640, 768), ("BSF", 128, 256), s1, A.is_gt)
+    tt(("HB", 0, 128), ("HOLD", 0, 128), ("HE", 0, 128), A.add)
+    scan(("LS", 0, 192), ("CH", 384, 576), ("CH", 576, 768), 0.0, A.add, A.add)
+    copy(("GOFF", 0, 4 * (N - 1)), ("GO", 0, 4 * (N - 1)))
+    for h, col in ((0, ("LR", 0, 1)), (1, ("LS", 191, 192))):
+        ts2(("BX", 32 * h, 32 * h + 32), ("ZB", 0, 32), col, 256.0 if high else 1.0, A.subtract if high else A.add, A.add)
+
+    def quad(name, a, b, p, n=32):
+        return (name, a, b, 1, p, p + n)
+
+    for a in range(4):
+        turn(quad("LRF", 64 * a, 64 * a + 64, 32 * a), quad("BX", 0, 64, 32 * a))
+    for a in range(4):
+        c = (64 * a, 64 * a + 64)
+        (copy if a < 2 else scopy)(quad("LRF", *c, 32 * (a ^ 1)), quad("LRF", *c, 32 * a))
+    copy(quad("LRF", 0, 128, 64, 64), quad("LRF", 0, 128, 0, 64))
+    scopy(quad("LRF", 128, 256, 0, 64), quad("LRF", 128, 256, 64, 64))
+    for a in (0, 128):
+        hold16(("LH", a, a + 128), ("LRF", a, a + 128))
+    for a in (0, 128):
+        take16(("LU", a // 16, a // 16 + 8), ("LH", a, a + 128), 1.0)
+    vput(("INV", 0, 256), ("LU", 0, 16), ("JC", 0, 256))
+    best = 128 if high else 0
+    a, z = (0, 128) if high else (128, 0)
+    hold16(("NH", 0, 128), ("INV", best, best + 128))
+    take16(("NN", 0, 8), ("NH", 0, 128), 1.0)
+    own, got = window("W1", a, a + 128), window("W1", z, z + 128)
+    pick_columns(own, window("X", 0, 256), ("NN", 0, 8))
+
+    mate = rank ^ 1
+    exchange(mate, own, own, "arr1")
+    arrive(got, "arr1")
+    mm(("BA", 0, 128), *U, *own)
+    iota(("CB", 0, 128), [[-32 if high else 32, 4], [0, 32]], 128 if high else 1, 0)
+    iota(("VC", 0, 128), [[256, 128]], 256 * (ZC + 1) - 1, 0)
+    iota(("CT", 256, 1280), [[0, 4], [1, 256]], 0, 0)
+    for o in range(O):
+        hold("y", [("XQ", 0, 256)], [])
+        load("y", ("WT", 512 * o, 512 * o + 512), T.w[:, 512 * o:512 * o + 512], "dw%d" % o)
+    half = OTH // 2
+    vpick(("EX0", 0, half), ("SCR", 0, 16), ("GOFF", 0, half // 16))
+    spick(("EX0", half, OTH), ("SCR", 0, 16), ("GOFF", half // 16, OTH // 16))
+    turn(("ST", 0, 128), ("BA", 0, 128))
+    turn(("EX", 0, half), ("EX0", 0, half))
+    turn(("EX", half, OTH), ("EX0", half, OTH))
+    scopy(("SW", 0, 128), ("BA", 0, 128))
+    low = 64 * rank
+    for c in range(4):
+        s = ("ST", 32 * c, 32 * c + 1)
+        if low:
+            ts(("CM", OTH * c, OTH * c + low), ("EX", 0, low), s, A.is_ge)
+        if low < OTH:
+            ts(("CM", OTH * c + low, OTH * c + OTH), ("EX", low, OTH), s, A.is_gt)
+        accum(("CM", OTH * c, OTH * c + OTH), ("PG", c, c + 1))
+    ts(("KCB", 0, 128), ("CB", 0, 128), ("PM", 0, 1), A.subtract if high else A.add)
+    tt(("VAL", 0, 128), ("VC", 0, 128), ("INV", best, best + 128), A.add)
+    fill(("E1", 0, 256), 256.0)
+    ts(("BASE", 0, 128), ("J128", 0, 128), a + 1.0, A.add)
+    ts(("K128", 0, 4), ("KCB", 0, 128, 32), 128.0, A.add)
+    copy(quad("X1", 0, 4, 0, 64), quad("PG", 0, 4, 64, 64))
+    scopy(quad("X1", 0, 4, 64, 64), quad("PG", 0, 4, 0, 64))
+    mm(("BB", 0, 128), *U, *got)
+    tt(("P2", 0, 4), ("PG", 0, 4), ("X1", 0, 4), A.add)
+    tt(("G", 0, 128), ("BB", 0, 128), ("SW", 0, 128), A.is_ge if high else A.is_gt)
+    for i in range(4):
+        (copy if i < 2 else scopy)(quad("X2", 0, 4, 32 * i), quad("P2", 0, 4, 32 * (i ^ 1)))
+    ts(("GX", 0, 128), ("G", 0, 128), 128.0 if high else -128.0, A.mult)
+    tt(("P3", 0, 4), ("P2", 0, 4), ("X2", 0, 4), A.add)
+    tt(("FX", 0, 128), ("BASE", 0, 128), ("GX", 0, 128), A.add)
+    for c in range(4):
+        b = (32 * c, 32 * c + 32)
+        ts2(("BXG",) + b, ("KCB",) + b, ("P3", c, c + 1), ("K128", c, c + 1), A.add, A.min)
+    hold16(("FH", 0, 128), ("FX", 0, 128))
+    turn(("GFX", 0, 128), ("BXG", 0, 128))
+    take16(("LOF", 0, 8), ("FH", 0, 128), 1.0)
+    hold16(("GH", 0, 128), ("GFX", 0, 128))
+    S2, L2 = window("Z", ZC, ZC + 128), window("Z", ZC + 128, ZC + 256)
+    pick_columns(S2, window("W1", 0, 256), ("LOF", 0, 8))
+    take16(("LUG", 0, 8), ("GH", 0, 128), 1.0)
+    mate = rank ^ 2
+    exchange(mate, L2, S2, "arr2")
+    arrive(L2, "arr2")
+    vput(("E1", 0, 256), ("LUG", 0, 8), ("VAL", 0, 128))
+    hold16(("EH", 0, 128), ("E1", 0, 128))
+    take16(("LV4", 0, 8), ("EH", 0, 128), 256.0)
+    place = {0: 0, 2: 8, 1: 16, 3: 24}
+    spread([rank ^ d for d in (1, 2, 3)], [("LV4", place[d], place[d] + 8) for d in (1, 2, 3)], ("LV4", 0, 8), "num1")
+    arrive([("LV4", 8, 32)], "num1")
+    fill(("ZOFF", 0, 2), 256)
+    pick_columns(window("Z", 0, ZC), window("X", 0, 256 + ZC), ("ZOFF", 0, 1))
+    for o in range(O):
+        quant(("WQ", 128 * o, 128 * o + 128), ("WS", 128 * o, 128 * o + 128), ("WT", 512 * o, 512 * o + 512))
+    fill(("CT", 0, 256), 0.0)
+    for name, first in (("RTO", rank & 4), ("RTA", rank & 4 ^ 4)):
+        fill((name, 0, 256), 0.0)
+        for i in range(4):
+            fill((name, 256 * i + 256, 256 * i + 512), float(first + i))
+    copy(("VI", 0, 32), ("LV4", 0, 32))
+    tt(("MO", 0, 16), ("VI", 0, 16), ("VI", 16, 32), A.max)
+    ts(("AN", 0, 32), ("VI", 0, 32), 255, A.bitwise_and)
+    ts2(("FO", 0, 8), ("MO", 8, 16), 0.0, 256.0 * 128, A.is_gt, A.mult)
+    tt(("TM", 0, 8), ("MO", 0, 8), ("MO", 8, 16), A.add)
+    for d in (0, 1):
+        ts2(("GN", place[d], place[d] + 8), ("VI", place[d], place[d] + 8), 0.0, 256.0 * (((rank ^ d) & 3) + 1), A.is_gt, A.mult)
+    tt(("TC", 0, 8), ("TM", 0, 8), ("FO", 0, 8), A.add)
+    for d in (2, 3):
+        ts2(("GN", place[d], place[d] + 8), ("VI", place[d], place[d] + 8), 0.0, 256.0 * (((rank ^ d) & 3) + 1), A.is_gt, A.mult)
+    ts(("TK", 0, 8), ("TC", 0, 8), 8, A.arith_shift_right)
+    tt(("SN", 0, 32), ("AN", 0, 32), ("GN", 0, 32), A.add)
+    copy(("LC", 0, 8), ("TK", 0, 8))
+    tt(("SM", 0, 16), ("SN", 0, 16), ("SN", 16, 32), A.add)
+    V4, L4 = window("V4", 0, 128), window("L4", 0, 128)
+    pick_columns(V4, window("Z", 0, 256 + ZC), ("LC", 0, 8))
+    mate = rank ^ 4
+    exchange(mate, L4, V4, "arr3")
+    arrive(L4, "arr3")
+    tt(("NI", 0, 8), ("SM", 0, 8), ("SM", 8, 16), A.add)
+    copy(("LID", 0, 8), ("NI", 0, 8))
+    send(mate, ("LIA", 0, 8), ("LID", 0, 8), "num3")
+    arrive([("LIA", 0, 8)], "num3")
+    for o in range(O):
+        mm(("BY%d" % o, 0, 128), *window("W", 128 * o, 128 * o + 128), *V4, True, False)
+    vpick(("IDO", 0, 128), ("RTO", 0, 1280), ("LID", 0, 8))
+    spick(("IDO", 128, 256), ("CT", 0, 1280), ("LID", 0, 8))
+    for o in range(O):
+        mm(("BY%d" % o, 0, 128), *window("W", 128 * o, 128 * o + 128), *L4, False, True)
+    copy(("YB", 0, 128), ("BY0", 0, 128))
+    scopy(("YB", 128, 256), ("BY1", 0, 128))
+    do("y", lambda: g.sync.dma_start(T.y[:, :], ap(("YB", 0, 256))), [], [("YB", 0, 256)], "dy", 16)
+    vpick(("IDA", 0, 128), ("RTA", 0, 1280), ("LIA", 0, 8))
+    spick(("IDA", 128, 256), ("CT", 0, 1280), ("LIA", 0, 8))
+    tt(("IDB", 0, 256), ("IDO", 0, 256), ("IDA", 0, 256), A.add)
+    do("s", lambda: g.scalar.dma_start(T.id[:, :], T.IDB[0:1, 0:256]), [], [("IDB", 0, 256)], "did", 16)
+    late = ("t", "v", "s", "did", "dy")
+    for sem in sorted(x for x in total if x not in late) + list(late):
+        if known["g"].get(sem, 0) < total[sem]:
+            g.wait_ge(T.sem[sem], total[sem])

@@ -1,10 +1,11 @@
 from concourse.bass import DstId, RemoteDMATransfer
-from concourse.mybir import dt, AluOpType, ActivationFunctionType
+from concourse.mybir import dt, AluOpType, ActivationFunctionType, AxisListType
 
 N, T_COLS, K, O = 8, 256, 128, 2
 BF, F32, U16, I32, CODE, U8 = "bfloat16", "float32", "uint16", "int32", "float8_e4m3fn_x4", "uint8"
 OTH = 64 * (N - 1)
 ZC = 16
+ROUND = 2064
 
 
 def _sbuf(cols, dtype, names):
@@ -12,7 +13,7 @@ def _sbuf(cols, dtype, names):
 
 
 SCRATCH = {}
-SCRATCH.update(_sbuf(512, BF, "UT"))
+SCRATCH.update(_sbuf(512, BF, "UT INV EQ LS SG"))
 SCRATCH.update(_sbuf(1024 + 4 * ZC, BF, "XT"))
 SCRATCH.update(_sbuf(1024, BF, "WT"))
 SCRATCH.update(_sbuf(128, CODE, "UQ0 UQ V4Q L4Q"))
@@ -21,34 +22,38 @@ SCRATCH.update(_sbuf(256, CODE, "WQ W1Q"))
 SCRATCH.update(_sbuf(256, U8, "WS W1S"))
 SCRATCH.update(_sbuf(256 + ZC, CODE, "XQ ZQ"))
 SCRATCH.update(_sbuf(256 + ZC, U8, "XS ZS"))
-SCRATCH.update(_sbuf(8, U16, "UOFF NN LOF LUG LC LID LIA"))
+SCRATCH.update(_sbuf(8, U16, "UOFF NN LOF LUG LC"))
 SCRATCH.update(_sbuf(2, U16, "ZOFF"))
-SCRATCH.update(_sbuf(16, U16, "LU"))
+SCRATCH.update(_sbuf(4, U16, "LU"))
 SCRATCH.update(_sbuf(32, U16, "LV4"))
 SCRATCH.update(_sbuf(4 * (N - 1), U16, "GOFF"))
 SCRATCH.update(_sbuf(4 * (N - 1), BF, "GO"))
-SCRATCH.update(_sbuf(1, I32, "PIDX MI MJ"))
-SCRATCH.update(_sbuf(8, I32, "FO TM TC TK NI"))
-SCRATCH.update(_sbuf(16, I32, "MO SM"))
-SCRATCH.update(_sbuf(32, I32, "VI AN GN SN"))
-SCRATCH.update(_sbuf(1, F32, "MF PF MF1 SC0 SC LR PM"))
-SCRATCH.update(_sbuf(2, F32, "SCO"))
-SCRATCH.update(_sbuf(16, F32, "SCR"))
-SCRATCH.update(_sbuf(4, F32, "PG X1 P2 X2 P3 K128"))
-SCRATCH.update(_sbuf(256, BF, "JC TRI EQ LRF LH INV IDO IDA"))
-SCRATCH.update(_sbuf(128, BF, "J128 TMOD HOLD HE HB BASE ZB G GX FX FH NH CB KCB BXG GFX GH"))
-SCRATCH.update(_sbuf(1280, BF, "RTO RTA CT"))
-SCRATCH.update(_sbuf(768, BF, "CH"))
-SCRATCH.update(_sbuf(192, BF, "LS"))
-SCRATCH.update(_sbuf(64, BF, "BX"))
-SCRATCH.update(_sbuf(4 * OTH, BF, "CM"))
+SCRATCH.update(_sbuf(1, I32, "PIDX"))
+SCRATCH.update(_sbuf(3, I32, "PI"))
+SCRATCH.update(_sbuf(3, F32, "PF"))
+SCRATCH.update(_sbuf(1, F32, "MF1 SC0 SC SCB PS"))
+SCRATCH.update(_sbuf(2, F32, "SCO SA C2 PG IDO IDA"))
+SCRATCH.update(_sbuf(2, BF, "RQ SH"))
+SCRATCH.update(_sbuf(8, BF, "T1 T2 T3"))
+SCRATCH.update(_sbuf(8, I32, "MM COL"))
+SCRATCH.update(_sbuf(8, F32, "CD"))
+SCRATCH.update(_sbuf(16, F32, "SCR DD"))
+SCRATCH.update(_sbuf(32, F32, "VI FL FR RKD RK DG B16 IDB"))
+SCRATCH.update(_sbuf(128, F32, "IDT"))
+SCRATCH.update(_sbuf(4, F32, "P2 P3 K128"))
+SCRATCH.update(_sbuf(64, BF, "JC JC0"))
+SCRATCH.update(_sbuf(256, BF, "J256 TR"))
+SCRATCH.update(_sbuf(384, BF, "MD"))
+SCRATCH.update(_sbuf(128, BF, "COLR TMOD HOLD HE HB BASE G FX FH CB KCB BXG GFX GH"))
+SCRATCH.update(_sbuf(4 * OTH + 128, BF, "CM"))
+SCRATCH.update(_sbuf(640, BF, "CA CS"))
 SCRATCH.update(_sbuf(OTH, F32, "EX0 EX"))
 SCRATCH.update(_sbuf(128, F32, "ST SW VC VAL EH"))
-SCRATCH.update(_sbuf(256, F32, "E1 YB IDB"))
-PSUM_NAMES = ["BSF", "BS0", "BS1", "BA", "BB", "BY0", "BY1"]
+SCRATCH.update(_sbuf(256, F32, "SF E1 YB"))
+PSUM_NAMES = ["BS0", "BS1", "BSG", "BB", "BY0", "BY1"]
 SCRATCH.update({n: ("psum", [128, 512], F32) for n in PSUM_NAMES})
 SEMAPHORES = ["v", "s", "t", "gc", "du", "dx0", "dx1", "dw0", "dw1", "dy", "did", "loc",
-              "arr1", "arr2", "arr3", "sc", "num1", "num3"]
+              "arr1", "arr2", "arr3", "sca", "scb", "num1", "num3"]
 
 
 def rank_program(g, core, T, topo):
@@ -108,6 +113,9 @@ def rank_program(g, core, T, topo):
         p, z = parts(r)
         return T[r[0]][p:z, r[1]:r[2]:r[3]]
 
+    def quad(name, a, b, p, n=32, step=1):
+        return (name, a, b, step, p, p + n)
+
     def words(r):
         return ap(r).bitcast(dt.uint32)
 
@@ -126,6 +134,9 @@ def rank_program(g, core, T, topo):
     def scan(out, a, b, init, op0, op1):
         do("v", lambda: g.vector.tensor_tensor_scan(ap(out), ap(a), ap(b), init, op0, op1), [out], [a, b])
 
+    def total_of(out, a):
+        do("v", lambda: g.vector.tensor_reduce(ap(out), ap(a), AxisListType.X, A.add), [out], [a])
+
     def turn(out, a):
         do("v", lambda: g.vector.transpose(ap(out), ap(a)), [out], [a])
 
@@ -134,6 +145,11 @@ def rank_program(g, core, T, topo):
 
     def scopy(out, a):
         do("s", lambda: g.scalar.activation(ap(out), ap(a), F.Copy), [out], [a])
+
+    def act(out, a, func, bias=0.0, scale=1.0, sums=None):
+        cols = [bias] if isinstance(bias, tuple) else []
+        do("s", lambda: g.scalar.activation(ap(out), ap(a), func, bias=ap(bias) if cols else bias, scale=scale,
+                                            accum_out=ap(sums) if sums else None), [out] + ([sums] if sums else []), [a] + cols)
 
     def vpick(out, win, off):
         do("v", lambda: g.vector.tensor_copy(ap(out), ap(win).indirect(ap(off))), [out], [win, off])
@@ -160,14 +176,11 @@ def rank_program(g, core, T, topo):
     def mm(out, wq, ws, xq, xs, start=True, stop=True):
         do("t", lambda: g.tensor.matmul_mx(ap(out), ap(wq), ap(ws), ap(xq), ap(xs), start, stop), [out], [wq, ws, xq, xs])
 
-    def accum(buf, out):
-        do("s", lambda: g.scalar.activation(ap(buf), ap(buf), F.Identity, accum_out=ap(out)), [buf, out], [buf])
-
     def hold16(tmp, x):
-        scan(tmp, ("HB", 0, tmp[2] - tmp[1]), x, 0.0, A.mult, A.max)
+        scan(tmp, ("HB", 0, 128), x, 0.0, A.mult, A.max)
 
-    def take16(out, tmp, less):
-        ts2(out, (tmp[0], tmp[1] + 15, tmp[2], 16), ("SC", 0, 1), less, A.mult, A.subtract)
+    def take16(out, tmp, less, scale="SC"):
+        ts2(out, (tmp[0], 15, 128, 16), (scale, 0, 1), less, A.mult, A.subtract)
 
     def load(q, out, src, sem):
         do(q, lambda: engines[q].dma_start(ap(out), src), [out], [], sem, 16)
@@ -204,6 +217,7 @@ def rank_program(g, core, T, topo):
         return (name + "Q", a, b), (name + "S", a, b)
 
     high = rank & 1
+    upper = rank & 2
 
     load("y", ("UT", 0, 8), T.u[:, 0:8], "du")
     load("s", ("XT", 0, 512), T.x[:, 0:512], "dx0")
@@ -212,184 +226,198 @@ def rank_program(g, core, T, topo):
     fill(("UT", 8, 512), 0.0)
     fill(("XT", 1024, 1024 + 4 * ZC), 0.0)
     fill(("UOFF", 0, 8), 0)
+    best = 256 if high else 0
+    fill(("MD", 0, 384), 1.0)
+    fill(("INV", best, best + 256), 0.0)
     iota(("PIDX", 0, 1), [[0, 1]], 0, 1)
-    iota(("J128", 0, 128), [[1, 128]], 0, 0)
     iota(("TMOD", 0, 128), [[0, 8], [1, 16]], 0, 0)
-    iota(("JC", 0, 256), [[32, 4], [128, 2], [1, 32]], 1, 0)
-    if rank:
-        iota(("GO", 0, 4 * rank), [[1, 2 * rank], [0, 2]], 0, 0)
-    if rank < N - 1:
-        iota(("GO", 4 * rank, 4 * (N - 1)), [[1, 2 * (N - 1 - rank)], [0, 2]], 2 * rank + 2, 0)
-    ts(("MI", 0, 1), ("PIDX", 0, 1), 15, A.bitwise_and)
-    ts(("MJ", 0, 1), ("PIDX", 0, 1), 31, A.bitwise_and)
-    copy(("PF", 0, 1), ("PIDX", 0, 1))
-    copy(("MF", 0, 1), ("MI", 0, 1))
-    copy(("PM", 0, 1), ("MJ", 0, 1))
-    for h in (0, 1):
-        ts(("TRI", 128 * h, 128 * h + 128), ("J128", 0, 128), ("PF", 0, 1), A.is_lt)
-
-    quant(("UQ0", 0, 128), ("US0", 0, 128), ("UT", 0, 512))
-    U = (("UQ", 0, 128), ("US", 0, 128))
-    pick_columns(U, (("UQ0", 0, 128), ("US0", 0, 128)), ("UOFF", 0, 8))
-    quant(("XQ", 0, 128), ("XS", 0, 128), ("XT", 0, 512))
-    quant(("XQ", 128, 256 + ZC), ("XS", 128, 256 + ZC), ("XT", 512, 1024 + 4 * ZC))
-    for h in (0, 1):
-        mm(("BY%d" % h, 0, 128), *window("X", 128 * h, 128 * h + 128), *U)
-        scopy(("SCO", h, h + 1), ("BY%d" % h, 0, 1))
-        if h == 0:
-            mm(("BS0", 0, 128), *window("X", 0, 128), *U)
-            mm(("BSF", 0, 256), *U, *window("X", 0, 256))
-    mm(("BS1", 0, 128), *window("X", 128, 256), *U)
-    others = [s for s in range(N) if s != rank]
-    spread(others, [("SCR", 2 * rank, 2 * rank + 2)] * (N - 1), ("SCO", 0, 2), "sc")
-    arrive([("SCR", 0, 16)], "sc")
-    fill(("ZB", 0, 128), 0.0)
-    ts(("MF1", 0, 1), ("MF", 0, 1), 1.0, A.add)
-    ts2(("SC0", 0, 1), ("MF", 0, 1), 15.0, 255.0 / 256.0, A.is_equal, A.mult)
-    ts(("HOLD", 0, 128), ("TMOD", 0, 128), ("MF", 0, 1), A.is_gt)
+    diag = ("MD", 128, 256)
+    do("g", lambda: g.affine_select(ap(diag), ap(diag), [[-1, 128]], A.not_equal, -1.0, 0, 1), [diag], [diag])
+    iota(("C2", 0, 2), [[16, 2]], (127 if high else 128) - ROUND, 0)
+    iota(("JC0", 0, 64), [[128, 2], [0, 2], [1, 16]], 0, 0)
+    iota(("GO", 0, 4 * (N - 1)), [[1, 2 * (N - 1)], [0, 2]], 0, 0)
+    for i, bits in enumerate((15, 31, 112)):
+        ts(("PI", i, i + 1), ("PIDX", 0, 1), bits, A.bitwise_and)
+    copy(("PF", 0, 3), ("PI", 0, 3))
+    MF, PM, P16 = ("PF", 0, 1), ("PF", 1, 2), ("PF", 2, 3)
+    act(("MF1", 0, 1), MF, F.Identity, 1.0)
+    act(("PS", 0, 1), PM, F.Identity, 0.0, -1.0 if high else 1.0)
+    act(("JC", 0, 64), ("JC0", 0, 64), F.Identity, P16)
+    ts(("HOLD", 0, 128), ("TMOD", 0, 128), MF, A.is_gt)
+    ts2(("SC0", 0, 1), MF, 15.0, 255.0 / 256.0, A.is_equal, A.mult)
     ts2(("HE", 0, 128), ("TMOD", 0, 128), ("MF1", 0, 1), 255.0, A.is_equal, A.mult)
-    ts(("SC", 0, 1), ("SC0", 0, 1), 1.0 / 256.0, A.add)
-
-    s0, s1 = ("BS0", 0, 1), ("BS1", 0, 1)
-    ts(("EQ", 0, 128), ("BSF", 0, 128), s0, A.is_equal)
-    ts(("EQ", 128, 256), ("BSF", 128, 256), s1, A.is_equal)
-    ts(("CH", 0, 256), ("BSF", 0, 256), s0, A.is_gt)
-    tt(("CH", 256, 512), ("EQ", 0, 256), ("TRI", 0, 256), A.mult)
-    accum(("CH", 0, 384), ("LR", 0, 1))
-    ts(("CH", 512, 640), ("BSF", 0, 128), s1, A.is_ge)
-    ts(("CH", 640, 768), ("BSF", 128, 256), s1, A.is_gt)
     tt(("HB", 0, 128), ("HOLD", 0, 128), ("HE", 0, 128), A.add)
-    scan(("LS", 0, 192), ("CH", 384, 576), ("CH", 576, 768), 0.0, A.add, A.add)
+    act(("SC", 0, 1), ("SC0", 0, 1), F.Identity, 1.0 / 256.0)
+    act(("SCB", 0, 1), ("SC0", 0, 1), F.Identity, 0.5, 128.0)
+
+    U0, U = (("UQ0", 0, 128), ("US0", 0, 128)), (("UQ", 0, 128), ("US", 0, 128))
+    quant(*U0, ("UT", 0, 512))
+    quant(("XQ", 0, 128), ("XS", 0, 128), ("XT", 0, 512))
+    pick_columns(U, U0, ("UOFF", 0, 8))
+    quant(("XQ", 128, 256 + ZC), ("XS", 128, 256 + ZC), ("XT", 512, 1024 + 4 * ZC))
+    def equal(h, part):
+        b = 256 * h + 128 * part
+        ts(("EQ", b, b + 128), ("BS%d" % part, 0, 128), ("SCO", h, h + 1), A.is_equal)
+
+    for h in (0, 1):
+        mm(("BY%d" % h, 0, 128), *window("X", 128 * h, 128 * h + 128), *U0)
+        (copy if h else scopy)(("SCO", h, h + 1), ("BY%d" % h, 0, 1))
+        mm(("BS%d" % h, 0, 128), *U, *window("X", 128 * h, 128 * h + 128))
+        if h == 0:
+            equal(0, 0)
+    mm(("BSG", 0, 256), *U, *window("X", 0, 256))
+    r4 = rank & 3
+    near = [rank ^ d for d in (1, 2, 3)]
+    spread(near, [("SCR", 2 * i, 2 * i + 2) for i in [r4 - (r4 > m & 3) for m in near]], ("SCO", 0, 2), "sca")
+    arrive([("SCR", 0, 6)], "sca")
+    spread([rank ^ d for d in (4, 5, 6, 7)], [("SCR", 6 + 2 * r4, 8 + 2 * r4)] * 4, ("SCO", 0, 2), "scb")
+    arrive([("SCR", 6, 14)], "scb")
+    sign = -1 if upper else 1
+    iota(("J256", 0, 256), [[sign, 256]], 0, 0)
+    iota(("CB", 0, 128), [[-32 if high else 32, 4], [0, 32]], 128 if high else 1, 0)
+    iota(("VC", 0, 128), [[-256 if upper else 256, 128]], 256 * (129 if upper else ZC + 1), 0)
+
+    for h, part in ((1, 0), (0, 1), (1, 1)):
+        equal(h, part)
+    for h in (0, 1):
+        act(("SG", 256 * h, 256 * h + 256), ("BSG", 0, 256), F.Sign, ("SCO", h, h + 1), -1.0, ("SA", h, h + 1))
+    scopy(("SF", 0, 256), ("BSG", 0, 256))
+    for h in (0, 1):
+        scan(("LS", 256 * h, 256 * h + 256), ("MD", 128 - 128 * h, 384 - 128 * h), ("EQ", 256 * h, 256 * h + 256), 0.0, A.mult, A.add)
+    for h in (0, 1):
+        ts2(("SH", h, h + 1), ("LS", 256 * h + 255, 256 * h + 256), ("SA", h, h + 1), 0.5 if high else -0.5, A.add, A.mult)
+    ts(("RQ", 0, 2), ("SH", 0, 2), (127.0 if high else 128.0) - 7.5 + ROUND, A.add)
+    for h in (0, 1):
+        ts2(("LU", 2 * h, 2 * h + 2), ("C2", 0, 2), ("RQ", h, h + 1), ("SH", h, h + 1), A.add, A.add)
+    vput(("INV", 0, 512), ("LU", 0, 4), ("JC", 0, 64))
     copy(("GOFF", 0, 4 * (N - 1)), ("GO", 0, 4 * (N - 1)))
-    for h, col in ((0, ("LR", 0, 1)), (1, ("LS", 191, 192))):
-        ts2(("BX", 32 * h, 32 * h + 32), ("ZB", 0, 32), col, 256.0 if high else 1.0, A.subtract if high else A.add, A.add)
-
-    def quad(name, a, b, p, n=32):
-        return (name, a, b, 1, p, p + n)
-
-    for a in range(4):
-        turn(quad("LRF", 64 * a, 64 * a + 64, 32 * a), quad("BX", 0, 64, 32 * a))
-    for a in range(4):
-        c = (64 * a, 64 * a + 64)
-        (copy if a < 2 else scopy)(quad("LRF", *c, 32 * (a ^ 1)), quad("LRF", *c, 32 * a))
-    copy(quad("LRF", 0, 128, 64, 64), quad("LRF", 0, 128, 0, 64))
-    scopy(quad("LRF", 128, 256, 0, 64), quad("LRF", 128, 256, 64, 64))
-    for a in (0, 128):
-        hold16(("LH", a, a + 128), ("LRF", a, a + 128))
-    for a in (0, 128):
-        take16(("LU", a // 16, a // 16 + 8), ("LH", a, a + 128), 1.0)
-    vput(("INV", 0, 256), ("LU", 0, 16), ("JC", 0, 256))
-    best = 128 if high else 0
     a, z = (0, 128) if high else (128, 0)
-    hold16(("NH", 0, 128), ("INV", best, best + 128))
-    take16(("NN", 0, 8), ("NH", 0, 128), 1.0)
+    turn(("TR", 0, 256), ("INV", best, best + 256))
+    tt(("T1", 0, 8), ("TR", 0, 256, 32), ("TR", 16, 256, 32), A.add)
+    tt(quad("T2", 0, 8, 0, 64), quad("T1", 0, 8, 0, 64), quad("T1", 0, 8, 64, 64), A.add)
+    for p in (0, 32):
+        tt(quad("T3", 0, 8, p), quad("T2", 0, 8, 0), quad("T2", 0, 8, 32), A.add)
+    for p in (0, 64):
+        copy(quad("NN", 0, 8, p, 64), quad("T3", 0, 8, 0, 64))
+    act(("BASE", 0, 128), ("J256", 0, 128), F.Identity, 129.0 / 128.0, sign / 128.0)
+    act(("E1", 0, 128), ("J256", 0, 128), F.Identity, 256.0, 0.0)
+    act(("KCB", 0, 128), ("CB", 0, 128), F.Identity, ("PS", 0, 1))
+    act(("K128", 0, 4), ("KCB", 0, 128, 32), F.Identity, 128.0)
     own, got = window("W1", a, a + 128), window("W1", z, z + 128)
     pick_columns(own, window("X", 0, 256), ("NN", 0, 8))
+    spick(("SW", 0, 128), ("SF", 0, 256), ("NN", 0, 8))
+    do("v", lambda: g.vector.tensor_tensor(ap(("VAL", 0, 128)), ap(("J256", 0, 256)).indirect(ap(("NN", 0, 8))), ap(("VC", 0, 128)), A.add),
+       [("VAL", 0, 128)], [("J256", 0, 256), ("NN", 0, 8), ("VC", 0, 128)])
+    turn(("ST", 0, 128), ("SW", 0, 128))
 
     mate = rank ^ 1
     exchange(mate, own, own, "arr1")
     arrive(got, "arr1")
-    mm(("BA", 0, 128), *U, *own)
-    iota(("CB", 0, 128), [[-32 if high else 32, 4], [0, 32]], 128 if high else 1, 0)
-    iota(("VC", 0, 128), [[256, 128]], 256 * (ZC + 1) - 1, 0)
-    iota(("CT", 256, 1280), [[0, 4], [1, 256]], 0, 0)
     for o in range(O):
         hold("y", [("XQ", 0, 256)], [])
         load("y", ("WT", 512 * o, 512 * o + 512), T.w[:, 512 * o:512 * o + 512], "dw%d" % o)
-    half = OTH // 2
-    vpick(("EX0", 0, half), ("SCR", 0, 16), ("GOFF", 0, half // 16))
-    spick(("EX0", half, OTH), ("SCR", 0, 16), ("GOFF", half // 16, OTH // 16))
-    turn(("ST", 0, 128), ("BA", 0, 128))
-    turn(("EX", 0, half), ("EX0", 0, half))
-    turn(("EX", half, OTH), ("EX0", half, OTH))
-    scopy(("SW", 0, 128), ("BA", 0, 128))
-    low = 64 * rank
+    iota(("B16", 0, 32), [[0, 4], [16, 8]], 0, 0)
+    iota(("RK", 0, 32), [[1, 4], [0, 8]], rank & 4, 0)
+    NEAR, MID = 192, 320
+    vpick(("EX0", 0, 96), ("SCR", 0, 6), ("GOFF", 0, 6))
+    spick(("EX0", 96, NEAR), ("SCR", 0, 6), ("GOFF", 6, 12))
+    for b, e in ((NEAR, MID), (MID, OTH)):
+        spick(("EX0", b, e), ("SCR", 0, 14), ("GOFF", b // 16, e // 16))
+    for b, e in ((0, 96), (96, NEAR)):
+        turn(("EX", b, e), ("EX0", b, e))
+
+    def beats(c, b, e, low, at):
+        s, o = ("ST", 32 * c, 32 * c + 1), OTH * c + at - b
+        if b < low:
+            ts(("CM", o + b, o + min(e, low)), ("EX", b, min(e, low)), s, A.is_ge)
+        if low < e:
+            ts(("CM", o + max(b, low), o + e), ("EX", max(b, low), e), s, A.is_gt)
+
+    def count(name, c, b, e, init=0.0):
+        m, end = (e - b) // 2, 160 * c + 160
+        o, first = OTH * c + b, ap(init) if init else init
+        regions = (name, end - m, end), ("CM", o, o + m), ("CM", o + m, o + 2 * m)
+        do("v", lambda: g.vector.tensor_tensor_scan(*[ap(r) for r in regions], first, A.add, A.add), [regions[0]],
+           list(regions[1:]) + ([init] if init else []))
+
     for c in range(4):
-        s = ("ST", 32 * c, 32 * c + 1)
-        if low:
-            ts(("CM", OTH * c, OTH * c + low), ("EX", 0, low), s, A.is_ge)
-        if low < OTH:
-            ts(("CM", OTH * c + low, OTH * c + OTH), ("EX", low, OTH), s, A.is_gt)
-        accum(("CM", OTH * c, OTH * c + OTH), ("PG", c, c + 1))
-    ts(("KCB", 0, 128), ("CB", 0, 128), ("PM", 0, 1), A.subtract if high else A.add)
-    tt(("VAL", 0, 128), ("VC", 0, 128), ("INV", best, best + 128), A.add)
-    fill(("E1", 0, 256), 256.0)
-    ts(("BASE", 0, 128), ("J128", 0, 128), a + 1.0, A.add)
-    ts(("K128", 0, 4), ("KCB", 0, 128, 32), 128.0, A.add)
-    copy(quad("X1", 0, 4, 0, 64), quad("PG", 0, 4, 64, 64))
-    scopy(quad("X1", 0, 4, 64, 64), quad("PG", 0, 4, 0, 64))
+        beats(c, 0, NEAR, 64 * r4, 0)
+    for c in range(3):
+        count("CA", c, 0, NEAR)
+    for b, e in ((NEAR, MID), (MID, OTH)):
+        turn(("EX", b, e), ("EX0", b, e))
+    far = OTH if rank & 4 else 0
+    t = ("CM", 3 * OTH + NEAR, 4 * OTH)
+    act(t, ("EX", NEAR, OTH), F.Sign, ("ST", 96, 97), -1.0)
+    act(t, t, F.Sign if far else F.Relu, 1.0 if far else 0.0, -1.0, ("PG", 0, 1))
+    for c in range(3):
+        beats(c, NEAR, OTH, far, NEAR)
+    for c in range(3):
+        count("CS", c, NEAR, OTH, ("CA", 160 * c + 159, 160 * c + 160))
+    count("CS", 3, 0, NEAR, ("PG", 0, 1))
     mm(("BB", 0, 128), *U, *got)
-    tt(("P2", 0, 4), ("PG", 0, 4), ("X1", 0, 4), A.add)
-    tt(("G", 0, 128), ("BB", 0, 128), ("SW", 0, 128), A.is_ge if high else A.is_gt)
-    for i in range(4):
-        (copy if i < 2 else scopy)(quad("X2", 0, 4, 32 * i), quad("P2", 0, 4, 32 * (i ^ 1)))
-    ts(("GX", 0, 128), ("G", 0, 128), 128.0 if high else -128.0, A.mult)
-    tt(("P3", 0, 4), ("P2", 0, 4), ("X2", 0, 4), A.add)
-    tt(("FX", 0, 128), ("BASE", 0, 128), ("GX", 0, 128), A.add)
+    tt(quad("P2", 0, 4, 0, 64), quad("CS", 159, 640, 0, 64, 160), quad("CS", 159, 640, 64, 64, 160), A.add)
+    tt(("G", 0, 128), ("BB", 0, 128), ("SW", 0, 128), A.is_lt if high else A.is_gt)
+    for p in (0, 32):
+        tt(quad("P3", 0, 4, p), quad("P2", 0, 4, 0), quad("P2", 0, 4, 32), A.add)
     for c in range(4):
-        b = (32 * c, 32 * c + 32)
-        ts2(("BXG",) + b, ("KCB",) + b, ("P3", c, c + 1), ("K128", c, c + 1), A.add, A.min)
+        b = (32 * c, 32 * c + 32, 0, 64)
+        ts2(quad("BXG", *b), quad("KCB", *b), quad("P3", c, c + 1, 0, 64), quad("K128", c, c + 1, 0, 64), A.add, A.min)
+    scan(("FX", 0, 128), ("BASE", 0, 128), ("G", 0, 128), 0.0, A.max, A.subtract)
+    turn(quad("GFX", 0, 128, 0, 64), quad("BXG", 0, 128, 0, 64))
     hold16(("FH", 0, 128), ("FX", 0, 128))
-    turn(("GFX", 0, 128), ("BXG", 0, 128))
-    take16(("LOF", 0, 8), ("FH", 0, 128), 1.0)
-    hold16(("GH", 0, 128), ("GFX", 0, 128))
-    S2, L2 = window("Z", ZC, ZC + 128), window("Z", ZC + 128, ZC + 256)
+    scan(quad("GH", 0, 128, 0, 64), quad("HB", 0, 128, 0, 64), quad("GFX", 0, 128, 0, 64), 0.0, A.mult, A.max)
+    take16(("LOF", 0, 8), ("FH", 0, 128), 1.0, "SCB")
+    for p in (0, 64):
+        ts2(quad("LUG", 0, 8, p, 64), quad("GH", 15, 128, 0, 64, 16), quad("SC", 0, 1, 0, 64), 1.0, A.mult, A.subtract)
+    z2 = 0 if upper else 128 + ZC
+    S2 = window("Z", z2, z2 + 128)
+    L2 = window("Z", 128 + ZC - z2, 256 + ZC - z2)
     pick_columns(S2, window("W1", 0, 256), ("LOF", 0, 8))
-    take16(("LUG", 0, 8), ("GH", 0, 128), 1.0)
-    mate = rank ^ 2
-    exchange(mate, L2, S2, "arr2")
-    arrive(L2, "arr2")
+    send(rank ^ 2, S2[0], S2[0], "arr2", codes=True)
     vput(("E1", 0, 256), ("LUG", 0, 8), ("VAL", 0, 128))
-    hold16(("EH", 0, 128), ("E1", 0, 128))
-    take16(("LV4", 0, 8), ("EH", 0, 128), 256.0)
-    place = {0: 0, 2: 8, 1: 16, 3: 24}
-    spread([rank ^ d for d in (1, 2, 3)], [("LV4", place[d], place[d] + 8) for d in (1, 2, 3)], ("LV4", 0, 8), "num1")
-    arrive([("LV4", 8, 32)], "num1")
     fill(("ZOFF", 0, 2), 256)
-    pick_columns(window("Z", 0, ZC), window("X", 0, 256 + ZC), ("ZOFF", 0, 1))
+    hold16(("EH", 0, 128), ("E1", 0, 128))
+    mine = ("LV4", 8 * (rank & 3), 8 * (rank & 3) + 8)
+    take16(mine, ("EH", 0, 128), 256.0)
+    spread([rank ^ d for d in (1, 2, 3)], [mine] * 3, mine, "num1")
+    arrive([("LV4", 8 * (rank & 3 ^ d), 8 * (rank & 3 ^ d) + 8) for d in (1, 2, 3)], "num1")
+    send(rank ^ 2, S2[1], S2[1], "arr2")
+    arrive(L2, "arr2")
+    pick_columns(window("Z", 128, 128 + ZC), window("X", 0, 256 + ZC), ("ZOFF", 0, 1))
     for o in range(O):
         quant(("WQ", 128 * o, 128 * o + 128), ("WS", 128 * o, 128 * o + 128), ("WT", 512 * o, 512 * o + 512))
-    fill(("CT", 0, 256), 0.0)
-    for name, first in (("RTO", rank & 4), ("RTA", rank & 4 ^ 4)):
-        fill((name, 0, 256), 0.0)
-        for i in range(4):
-            fill((name, 256 * i + 256, 256 * i + 512), float(first + i))
+    ts(("DG", 0, 32), ("B16", 0, 32), P16, A.is_equal)
+    fill(("IDB", 0, 32), 0.0)
+    tt(("RKD", 0, 32), ("RK", 0, 32), ("DG", 0, 32), A.mult)
     copy(("VI", 0, 32), ("LV4", 0, 32))
-    tt(("MO", 0, 16), ("VI", 0, 16), ("VI", 16, 32), A.max)
-    ts(("AN", 0, 32), ("VI", 0, 32), 255, A.bitwise_and)
-    ts2(("FO", 0, 8), ("MO", 8, 16), 0.0, 256.0 * 128, A.is_gt, A.mult)
-    tt(("TM", 0, 8), ("MO", 0, 8), ("MO", 8, 16), A.add)
-    for d in (0, 1):
-        ts2(("GN", place[d], place[d] + 8), ("VI", place[d], place[d] + 8), 0.0, 256.0 * (((rank ^ d) & 3) + 1), A.is_gt, A.mult)
-    tt(("TC", 0, 8), ("TM", 0, 8), ("FO", 0, 8), A.add)
-    for d in (2, 3):
-        ts2(("GN", place[d], place[d] + 8), ("VI", place[d], place[d] + 8), 0.0, 256.0 * (((rank ^ d) & 3) + 1), A.is_gt, A.mult)
-    ts(("TK", 0, 8), ("TC", 0, 8), 8, A.arith_shift_right)
-    tt(("SN", 0, 32), ("AN", 0, 32), ("GN", 0, 32), A.add)
-    copy(("LC", 0, 8), ("TK", 0, 8))
-    tt(("SM", 0, 16), ("SN", 0, 16), ("SN", 16, 32), A.add)
+    tt(("DD", 0, 16), ("VI", 0, 16), ("VI", 16, 32), A.subtract)
+    ts(("FL", 0, 32), ("VI", 0, 32), 0.0, A.is_gt)
+    tt(("MM", 0, 8), ("DD", 0, 8), ("DD", 8, 16), A.add)
+    tt(("FR", 0, 32), ("FL", 0, 32), ("RKD", 0, 32), A.mult)
+    ts2(("LC", 0, 8), ("MM", 0, 8), 256.0 * 128 - 127.5, 1.0 / 256.0, A.add, A.mult)
+    ts(("COL", 0, 8), ("MM", 0, 8), 255, A.bitwise_and)
     V4, L4 = window("V4", 0, 128), window("L4", 0, 128)
     pick_columns(V4, window("Z", 0, 256 + ZC), ("LC", 0, 8))
     mate = rank ^ 4
     exchange(mate, L4, V4, "arr3")
     arrive(L4, "arr3")
-    tt(("NI", 0, 8), ("SM", 0, 8), ("SM", 8, 16), A.add)
-    copy(("LID", 0, 8), ("NI", 0, 8))
-    send(mate, ("LIA", 0, 8), ("LID", 0, 8), "num3")
-    arrive([("LIA", 0, 8)], "num3")
+    tt(("CD", 0, 8), ("COL", 0, 8), ("DG", 0, 8), A.mult)
+    total_of(("IDO", 0, 1), ("FR", 0, 32))
+    total_of(("IDO", 1, 2), ("CD", 0, 8))
+    send(mate, ("IDA", 0, 2), ("IDO", 0, 2), "num3")
+    arrive([("IDA", 0, 2)], "num3")
     for o in range(O):
         mm(("BY%d" % o, 0, 128), *window("W", 128 * o, 128 * o + 128), *V4, True, False)
-    vpick(("IDO", 0, 128), ("RTO", 0, 1280), ("LID", 0, 8))
-    spick(("IDO", 128, 256), ("CT", 0, 1280), ("LID", 0, 8))
-    for o in range(O):
+    for o in (1, 0):
         mm(("BY%d" % o, 0, 128), *window("W", 128 * o, 128 * o + 128), *L4, False, True)
-    copy(("YB", 0, 128), ("BY0", 0, 128))
     scopy(("YB", 128, 256), ("BY1", 0, 128))
+    copy(("YB", 0, 128), ("BY0", 0, 128))
     do("y", lambda: g.sync.dma_start(T.y[:, :], ap(("YB", 0, 256))), [], [("YB", 0, 256)], "dy", 16)
-    vpick(("IDA", 0, 128), ("RTA", 0, 1280), ("LIA", 0, 8))
-    spick(("IDA", 128, 256), ("CT", 0, 1280), ("LIA", 0, 8))
-    tt(("IDB", 0, 256), ("IDO", 0, 256), ("IDA", 0, 256), A.add)
-    do("s", lambda: g.scalar.dma_start(T.id[:, :], T.IDB[0:1, 0:256]), [], [("IDB", 0, 256)], "did", 16)
+    tt(("IDB", 0, 2), ("IDO", 0, 2), ("IDA", 0, 2), A.add)
+    for a in range(4):
+        turn(quad("IDT", 32 * a, 32 * a + 32, 0), quad("IDB", 0, 32, 32 * a))
+    do("s", lambda: g.scalar.dma_start(T.id[:, :], T.IDT[0:2, 0:128]), [], [("IDT", 0, 128)], "did", 16)
     late = ("t", "v", "s", "did", "dy")
     for sem in sorted(x for x in total if x not in late) + list(late):
         if known["g"].get(sem, 0) < total[sem]:

@@ -25,35 +25,34 @@ SCRATCH.update(_sbuf(256 + ZC, U8, "XS ZS"))
 SCRATCH.update(_sbuf(8, U16, "UOFF NN LOF LUG LC"))
 SCRATCH.update(_sbuf(2, U16, "ZOFF"))
 SCRATCH.update(_sbuf(4, U16, "LU"))
-SCRATCH.update(_sbuf(32, U16, "LV4"))
 SCRATCH.update(_sbuf(4 * (N - 1), U16, "GOFF"))
 SCRATCH.update(_sbuf(4 * (N - 1), BF, "GO"))
 SCRATCH.update(_sbuf(1, I32, "PIDX"))
 SCRATCH.update(_sbuf(3, I32, "PI"))
-SCRATCH.update(_sbuf(3, F32, "PF"))
-SCRATCH.update(_sbuf(1, F32, "MF1 SC0 SC SCB PS"))
-SCRATCH.update(_sbuf(2, F32, "SCO SA C2 PG IDO IDA"))
-SCRATCH.update(_sbuf(2, BF, "RQ SH"))
-SCRATCH.update(_sbuf(8, BF, "T1 T2 T3"))
-SCRATCH.update(_sbuf(8, I32, "MM COL"))
-SCRATCH.update(_sbuf(8, F32, "CD"))
-SCRATCH.update(_sbuf(16, F32, "SCR DD"))
-SCRATCH.update(_sbuf(32, F32, "VI FL FR RKD RK DG B16 IDB"))
-SCRATCH.update(_sbuf(128, F32, "IDT"))
-SCRATCH.update(_sbuf(4, F32, "P2 P3 K128"))
+SCRATCH.update(_sbuf(3, F32, "PF SA"))
+SCRATCH.update(_sbuf(1, F32, "MF1 SC0 SC SCB SCS PS NEG PG"))
+SCRATCH.update(_sbuf(2, F32, "SCO C2"))
+SCRATCH.update(_sbuf(2, BF, "RQ SH IDM IDR IDO IDA"))
+SCRATCH.update(_sbuf(8, BF, "T1 T2 T3 IDN MM"))
+SCRATCH.update(_sbuf(16, F32, "SCR"))
+SCRATCH.update(_sbuf(16, BF, "DD"))
+SCRATCH.update(_sbuf(32, BF, "LV4 DT"))
+SCRATCH.update(_sbuf(32, F32, "IDB KC3"))
+SCRATCH.update(_sbuf(4, F32, "P2 P3 K0 K1 K128"))
 SCRATCH.update(_sbuf(64, BF, "JC JC0"))
-SCRATCH.update(_sbuf(256, BF, "J256 TR"))
+SCRATCH.update(_sbuf(256, BF, "J256 TR E1 E2"))
 SCRATCH.update(_sbuf(384, BF, "MD"))
-SCRATCH.update(_sbuf(128, BF, "COLR TMOD HOLD HE HB BASE G FX FH CB KCB BXG GFX GH"))
-SCRATCH.update(_sbuf(4 * OTH + 128, BF, "CM"))
-SCRATCH.update(_sbuf(640, BF, "CA CS"))
+SCRATCH.update(_sbuf(128, BF, "COLR TMOD HOLD HE HB BASE G FX FH KCB BXG GFX GH VAL EH"))
+SCRATCH.update(_sbuf(3 * OTH, BF, "CM"))
+SCRATCH.update(_sbuf(480, BF, "CA CS"))
 SCRATCH.update(_sbuf(OTH, F32, "EX0 EX"))
-SCRATCH.update(_sbuf(128, F32, "ST SW VC VAL EH"))
-SCRATCH.update(_sbuf(256, F32, "SF E1 YB"))
-PSUM_NAMES = ["BS0", "BS1", "BSG", "BB", "BY0", "BY1"]
+SCRATCH.update(_sbuf(OTH + 1, F32, "TS"))
+SCRATCH.update(_sbuf(128, F32, "ST SW IDT"))
+SCRATCH.update(_sbuf(256, F32, "SF YB"))
+PSUM_NAMES = ["BS0", "BS1", "BG0", "BG1", "BSG", "BB", "BY0", "BY1"]
 SCRATCH.update({n: ("psum", [128, 512], F32) for n in PSUM_NAMES})
 SEMAPHORES = ["v", "s", "t", "gc", "du", "dx0", "dx1", "dw0", "dw1", "dy", "did", "loc",
-              "arr1", "arr2", "arr3", "sca", "scb", "num1", "num3"]
+              "arr1", "arr2", "arr3", "sca", "scb", "num1", "num2", "num3"]
 
 
 def rank_program(g, core, T, topo):
@@ -132,10 +131,11 @@ def rank_program(g, core, T, topo):
         do("v", lambda: g.vector.tensor_tensor(ap(out), ap(a), ap(b), op), [out], [a, b])
 
     def scan(out, a, b, init, op0, op1):
-        do("v", lambda: g.vector.tensor_tensor_scan(ap(out), ap(a), ap(b), init, op0, op1), [out], [a, b])
+        cols = [init] if isinstance(init, tuple) else []
+        do("v", lambda: g.vector.tensor_tensor_scan(ap(out), ap(a), ap(b), ap(init) if cols else init, op0, op1), [out], [a, b] + cols)
 
-    def total_of(out, a):
-        do("v", lambda: g.vector.tensor_reduce(ap(out), ap(a), AxisListType.X, A.add), [out], [a])
+    def total_of(out, a, op=A.add):
+        do("v", lambda: g.vector.tensor_reduce(ap(out), ap(a), AxisListType.X, op), [out], [a])
 
     def turn(out, a):
         do("v", lambda: g.vector.transpose(ap(out), ap(a)), [out], [a])
@@ -236,6 +236,9 @@ def rank_program(g, core, T, topo):
     iota(("C2", 0, 2), [[16, 2]], (127 if high else 128) - ROUND, 0)
     iota(("JC0", 0, 64), [[128, 2], [0, 2], [1, 16]], 0, 0)
     iota(("GO", 0, 4 * (N - 1)), [[1, 2 * (N - 1)], [0, 2]], 0, 0)
+    iota(("K0", 0, 4), [[-32 if high else 32, 4]], 128 if high else 1, 0)
+    sign = -1 if upper else 1
+    iota(("J256", 0, 256), [[1, 256]], 1, 0)
     for i, bits in enumerate((15, 31, 112)):
         ts(("PI", i, i + 1), ("PIDX", 0, 1), bits, A.bitwise_and)
     copy(("PF", 0, 3), ("PI", 0, 3))
@@ -247,43 +250,50 @@ def rank_program(g, core, T, topo):
     ts2(("SC0", 0, 1), MF, 15.0, 255.0 / 256.0, A.is_equal, A.mult)
     ts2(("HE", 0, 128), ("TMOD", 0, 128), ("MF1", 0, 1), 255.0, A.is_equal, A.mult)
     tt(("HB", 0, 128), ("HOLD", 0, 128), ("HE", 0, 128), A.add)
-    act(("SC", 0, 1), ("SC0", 0, 1), F.Identity, 1.0 / 256.0)
-    act(("SCB", 0, 1), ("SC0", 0, 1), F.Identity, 0.5, 128.0)
+    ts(("SC", 0, 1), ("SC0", 0, 1), 1.0 / 256.0, A.add)
+    ts2(("SCB", 0, 1), ("SC0", 0, 1), 1.0 / 256.0, 128.0, A.add, A.mult)
+    ts2(("SCS", 0, 1), ("SC0", 0, 1), 1.0 / 256.0, float(sign), A.add, A.mult)
 
     U0, U = (("UQ0", 0, 128), ("US0", 0, 128)), (("UQ", 0, 128), ("US", 0, 128))
     quant(*U0, ("UT", 0, 512))
     quant(("XQ", 0, 128), ("XS", 0, 128), ("XT", 0, 512))
     pick_columns(U, U0, ("UOFF", 0, 8))
     quant(("XQ", 128, 256 + ZC), ("XS", 128, 256 + ZC), ("XT", 512, 1024 + 4 * ZC))
+
     def equal(h, part):
         b = 256 * h + 128 * part
-        ts(("EQ", b, b + 128), ("BS%d" % part, 0, 128), ("SCO", h, h + 1), A.is_equal)
+        if h:
+            ts(("EQ", b, b + 128), ("BS%d" % part, 0, 128), ("BY1", 0, 1), A.is_equal)
+        else:
+            ts2(("EQ", b, b + 128), ("BS%d" % part, 0, 128), ("NEG", 0, 1), 0.0, A.add, A.is_equal)
 
     for h in (0, 1):
-        mm(("BY%d" % h, 0, 128), *window("X", 128 * h, 128 * h + 128), *U0)
+        x = window("X", 128 * h, 128 * h + 128)
+        mm(("BY%d" % h, 0, 128), *x, *U0)
+        if h == 0:
+            act(("NEG", 0, 1), ("BY0", 0, 1), F.Identity, 0.0, -1.0)
         (copy if h else scopy)(("SCO", h, h + 1), ("BY%d" % h, 0, 1))
-        mm(("BS%d" % h, 0, 128), *U, *window("X", 128 * h, 128 * h + 128))
+        for bank in (("BG1", "BS1") if h else ("BS0", "BG0")):
+            mm((bank, 0, 128), *U, *x)
         if h == 0:
             equal(0, 0)
+            act(("SG", 0, 128), ("BG0", 0, 128), F.Sign, ("NEG", 0, 1), 1.0, ("SA", 2, 3))
     mm(("BSG", 0, 256), *U, *window("X", 0, 256))
-    r4 = rank & 3
+    r4, far = rank & 3, rank & 4
     near = [rank ^ d for d in (1, 2, 3)]
-    spread(near, [("SCR", 2 * i, 2 * i + 2) for i in [r4 - (r4 > m & 3) for m in near]], ("SCO", 0, 2), "sca")
+    spread(near, [("SCR", 2 * i, 2 * i + 2) for i in [(r4 - m - 1) % 4 if far else r4 - (r4 > m) for m in near]], ("SCO", 0, 2), "sca")
     arrive([("SCR", 0, 6)], "sca")
     spread([rank ^ d for d in (4, 5, 6, 7)], [("SCR", 6 + 2 * r4, 8 + 2 * r4)] * 4, ("SCO", 0, 2), "scb")
     arrive([("SCR", 6, 14)], "scb")
-    sign = -1 if upper else 1
-    iota(("J256", 0, 256), [[sign, 256]], 0, 0)
-    iota(("CB", 0, 128), [[-32 if high else 32, 4], [0, 32]], 128 if high else 1, 0)
-    iota(("VC", 0, 128), [[-256 if upper else 256, 128]], 256 * (129 if upper else ZC + 1), 0)
 
     for h, part in ((1, 0), (0, 1), (1, 1)):
         equal(h, part)
-    for h in (0, 1):
-        act(("SG", 256 * h, 256 * h + 256), ("BSG", 0, 256), F.Sign, ("SCO", h, h + 1), -1.0, ("SA", h, h + 1))
+    act(("SG", 128, 256), ("BG1", 0, 128), F.Sign, ("SCO", 0, 1), -1.0, ("SA", 0, 1))
+    act(("SG", 256, 512), ("BSG", 0, 256), F.Sign, ("SCO", 1, 2), -1.0, ("SA", 1, 2))
     scopy(("SF", 0, 256), ("BSG", 0, 256))
     for h in (0, 1):
-        scan(("LS", 256 * h, 256 * h + 256), ("MD", 128 - 128 * h, 384 - 128 * h), ("EQ", 256 * h, 256 * h + 256), 0.0, A.mult, A.add)
+        scan(("LS", 256 * h, 256 * h + 256), ("MD", 128 - 128 * h, 384 - 128 * h), ("EQ", 256 * h, 256 * h + 256),
+             0.0 if h else ("SA", 2, 3), A.mult, A.add)
     for h in (0, 1):
         ts2(("SH", h, h + 1), ("LS", 256 * h + 255, 256 * h + 256), ("SA", h, h + 1), 0.5 if high else -0.5, A.add, A.mult)
     ts(("RQ", 0, 2), ("SH", 0, 2), (127.0 if high else 128.0) - 7.5 + ROUND, A.add)
@@ -299,70 +309,79 @@ def rank_program(g, core, T, topo):
         tt(quad("T3", 0, 8, p), quad("T2", 0, 8, 0), quad("T2", 0, 8, 32), A.add)
     for p in (0, 64):
         copy(quad("NN", 0, 8, p, 64), quad("T3", 0, 8, 0, 64))
-    act(("BASE", 0, 128), ("J256", 0, 128), F.Identity, 129.0 / 128.0, sign / 128.0)
-    act(("E1", 0, 128), ("J256", 0, 128), F.Identity, 256.0, 0.0)
-    act(("KCB", 0, 128), ("CB", 0, 128), F.Identity, ("PS", 0, 1))
-    act(("K128", 0, 4), ("KCB", 0, 128, 32), F.Identity, 128.0)
+    act(("K1", 0, 4), ("K0", 0, 4), F.Identity, ("PS", 0, 1))
+    act(("BASE", 0, 128), ("J256", 0, 128), F.Identity, 1.0, 1.0 / 128.0)
+    act(("E1", 0, 128), ("J256", 0, 128), F.Identity, 1.0, 0.0)
+    act(("VAL", 0, 128), ("J256", 0, 128), F.Identity, 130.0 if upper else float(ZC), float(sign))
+    for c in range(4):
+        act(("KCB", 32 * c, 32 * c + 32), ("J256", 0, 32), F.Identity, ("K1", c, c + 1), 0.0)
+    act(("K128", 0, 4), ("K1", 0, 4), F.Identity, 128.0)
+    if far:
+        act(("KC3", 0, 32), ("KCB", 96, 128), F.Identity, 4.0 * OTH)
     own, got = window("W1", a, a + 128), window("W1", z, z + 128)
-    pick_columns(own, window("X", 0, 256), ("NN", 0, 8))
+    NEAR, MID = 192, 320
+    cut = 64 * (3 - r4 if far else r4)
+    split = 64 if cut == 64 else 128
+    vpick(("EX0", 0, NEAR), ("SCR", 0, 6), ("GOFF", 0, NEAR // 16))
     spick(("SW", 0, 128), ("SF", 0, 256), ("NN", 0, 8))
-    do("v", lambda: g.vector.tensor_tensor(ap(("VAL", 0, 128)), ap(("J256", 0, 256)).indirect(ap(("NN", 0, 8))), ap(("VC", 0, 128)), A.add),
-       [("VAL", 0, 128)], [("J256", 0, 256), ("NN", 0, 8), ("VC", 0, 128)])
+    pick_columns(own, window("X", 0, 256), ("NN", 0, 8))
+    turn(("EX", 0, split), ("EX0", 0, split))
     turn(("ST", 0, 128), ("SW", 0, 128))
+    turn(("EX", split, NEAR), ("EX0", split, NEAR))
 
     mate = rank ^ 1
     exchange(mate, own, own, "arr1")
     arrive(got, "arr1")
     for o in range(O):
-        hold("y", [("XQ", 0, 256)], [])
+        hold("y", [("XT", 0, 512)], [])
         load("y", ("WT", 512 * o, 512 * o + 512), T.w[:, 512 * o:512 * o + 512], "dw%d" % o)
-    iota(("B16", 0, 32), [[0, 4], [16, 8]], 0, 0)
-    iota(("RK", 0, 32), [[1, 4], [0, 8]], rank & 4, 0)
-    NEAR, MID = 192, 320
-    vpick(("EX0", 0, 96), ("SCR", 0, 6), ("GOFF", 0, 6))
-    spick(("EX0", 96, NEAR), ("SCR", 0, 6), ("GOFF", 6, 12))
     for b, e in ((NEAR, MID), (MID, OTH)):
         spick(("EX0", b, e), ("SCR", 0, 14), ("GOFF", b // 16, e // 16))
-    for b, e in ((0, 96), (96, NEAR)):
-        turn(("EX", b, e), ("EX0", b, e))
+    ops = (A.is_gt, A.is_ge) if far else (A.is_ge, A.is_gt)
 
-    def beats(c, b, e, low, at):
-        s, o = ("ST", 32 * c, 32 * c + 1), OTH * c + at - b
-        if b < low:
-            ts(("CM", o + b, o + min(e, low)), ("EX", b, min(e, low)), s, A.is_ge)
-        if low < e:
-            ts(("CM", o + max(b, low), o + e), ("EX", max(b, low), e), s, A.is_gt)
+    def beats(c, b, e):
+        s, o = ("ST", 32 * c, 32 * c + 1), OTH * c
+        if b < cut:
+            ts(("CM", o + b, o + min(e, cut)), ("EX", b, min(e, cut)), s, ops[0])
+        if max(b, cut) < e:
+            ts(("CM", o + max(b, cut), o + e), ("EX", max(b, cut), e), s, ops[1])
 
     def count(name, c, b, e, init=0.0):
         m, end = (e - b) // 2, 160 * c + 160
-        o, first = OTH * c + b, ap(init) if init else init
-        regions = (name, end - m, end), ("CM", o, o + m), ("CM", o + m, o + 2 * m)
-        do("v", lambda: g.vector.tensor_tensor_scan(*[ap(r) for r in regions], first, A.add, A.add), [regions[0]],
-           list(regions[1:]) + ([init] if init else []))
+        o = OTH * c + b
+        scan((name, end - m, end), ("CM", o, o + m), ("CM", o + m, o + 2 * m), init, A.add, A.add)
 
-    for c in range(4):
-        beats(c, 0, NEAR, 64 * r4, 0)
-    for c in range(3):
-        count("CA", c, 0, NEAR)
+    way = 1.0 if far else -1.0
+    act(("TS", 0, NEAR), ("EX", 0, NEAR), F.Sign, ("ST", 96, 97), -1.0)
+    if cut:
+        act(("TS", 0, cut), ("TS", 0, cut), F.Sign, way, 1.0, ("TS", OTH, OTH + 1))
+    beats(0, 0, split)
+    beats(0, split, NEAR)
+    for c in (1, 2):
+        beats(c, 0, NEAR)
     for b, e in ((NEAR, MID), (MID, OTH)):
         turn(("EX", b, e), ("EX0", b, e))
-    far = OTH if rank & 4 else 0
-    t = ("CM", 3 * OTH + NEAR, 4 * OTH)
-    act(t, ("EX", NEAR, OTH), F.Sign, ("ST", 96, 97), -1.0)
-    act(t, t, F.Sign if far else F.Relu, 1.0 if far else 0.0, -1.0, ("PG", 0, 1))
     for c in range(3):
-        beats(c, NEAR, OTH, far, NEAR)
+        count("CA", c, 0, NEAR)
+    act(("TS", NEAR, OTH), ("EX", NEAR, OTH), F.Sign, ("ST", 96, 97), -1.0)
+    rest = ("TS", cut, OTH + 1 if cut else OTH)
+    act(rest, rest, F.Relu, 0.0, way, ("PG", 0, 1))
+    spick(("COLR", 0, 128), ("J256", 0, 256), ("NN", 0, 8))
+    act(("E2", 0, 128), ("J256", 0, 128), F.Identity, 0.0, 0.0)
+    for c in range(3):
+        beats(c, NEAR, OTH)
     for c in range(3):
         count("CS", c, NEAR, OTH, ("CA", 160 * c + 159, 160 * c + 160))
-    count("CS", 3, 0, NEAR, ("PG", 0, 1))
     mm(("BB", 0, 128), *U, *got)
-    tt(quad("P2", 0, 4, 0, 64), quad("CS", 159, 640, 0, 64, 160), quad("CS", 159, 640, 64, 64, 160), A.add)
-    tt(("G", 0, 128), ("BB", 0, 128), ("SW", 0, 128), A.is_lt if high else A.is_gt)
+    tt(quad("P2", 3, 4, 0, 64), quad("PG", 0, 1, 0, 64), quad("PG", 0, 1, 64, 64), A.add)
+    tt(quad("P2", 0, 3, 0, 64), quad("CS", 159, 480, 0, 64, 160), quad("CS", 159, 480, 64, 64, 160), A.add)
     for p in (0, 32):
         tt(quad("P3", 0, 4, p), quad("P2", 0, 4, 0), quad("P2", 0, 4, 32), A.add)
+    tt(("G", 0, 128), ("BB", 0, 128), ("SW", 0, 128), A.is_lt if high else A.is_gt)
     for c in range(4):
         b = (32 * c, 32 * c + 32, 0, 64)
-        ts2(quad("BXG", *b), quad("KCB", *b), quad("P3", c, c + 1, 0, 64), quad("K128", c, c + 1, 0, 64), A.add, A.min)
+        first, op = (quad("KC3", 0, 32, 0, 64), A.subtract) if far and c == 3 else (quad("KCB", *b), A.add)
+        ts2(quad("BXG", *b), first, quad("P3", c, c + 1, 0, 64), quad("K128", c, c + 1, 0, 64), op, A.min)
     scan(("FX", 0, 128), ("BASE", 0, 128), ("G", 0, 128), 0.0, A.max, A.subtract)
     turn(quad("GFX", 0, 128, 0, 64), quad("BXG", 0, 128, 0, 64))
     hold16(("FH", 0, 128), ("FX", 0, 128))
@@ -378,33 +397,34 @@ def rank_program(g, core, T, topo):
     vput(("E1", 0, 256), ("LUG", 0, 8), ("VAL", 0, 128))
     fill(("ZOFF", 0, 2), 256)
     hold16(("EH", 0, 128), ("E1", 0, 128))
-    mine = ("LV4", 8 * (rank & 3), 8 * (rank & 3) + 8)
-    take16(mine, ("EH", 0, 128), 256.0)
-    spread([rank ^ d for d in (1, 2, 3)], [mine] * 3, mine, "num1")
-    arrive([("LV4", 8 * (rank & 3 ^ d), 8 * (rank & 3 ^ d) + 8) for d in (1, 2, 3)], "num1")
+    mine = ("LV4", 8 * r4, 8 * r4 + 8)
+    take16(mine, ("EH", 0, 128), float(sign), "SCS")
+    spread(near, [mine] * 3, mine, "num1")
+    arrive([("LV4", 8 * (m & 3), 8 * (m & 3) + 8) for m in near], "num1")
     send(rank ^ 2, S2[1], S2[1], "arr2")
     arrive(L2, "arr2")
+    vput(("E2", 0, 256), ("LUG", 0, 8), ("COLR", 0, 128))
     pick_columns(window("Z", 128, 128 + ZC), window("X", 0, 256 + ZC), ("ZOFF", 0, 1))
+    for a in range(4):
+        turn(quad("DT", 0, 32, 32 * a), quad("E2", 32 * a, 32 * a + 32, 32 * a))
+    ts2(("IDM", 0, 1), ("DT", 0, 1), 0.0, float(rank), A.is_gt, A.mult)
+    ts2(("IDM", 1, 2), ("DT", 0, 1), 1.0, 0.0, A.subtract, A.max)
+    spread(near, [("IDN", 2 * d, 2 * d + 2) for d in range(3)], ("IDM", 0, 2), "num2")
+    arrive([("IDN", 0, 6)], "num2")
     for o in range(O):
         quant(("WQ", 128 * o, 128 * o + 128), ("WS", 128 * o, 128 * o + 128), ("WT", 512 * o, 512 * o + 512))
-    ts(("DG", 0, 32), ("B16", 0, 32), P16, A.is_equal)
     fill(("IDB", 0, 32), 0.0)
-    tt(("RKD", 0, 32), ("RK", 0, 32), ("DG", 0, 32), A.mult)
-    copy(("VI", 0, 32), ("LV4", 0, 32))
-    tt(("DD", 0, 16), ("VI", 0, 16), ("VI", 16, 32), A.subtract)
-    ts(("FL", 0, 32), ("VI", 0, 32), 0.0, A.is_gt)
+    tt(("DD", 0, 16), ("LV4", 0, 16), ("LV4", 16, 32), A.add)
     tt(("MM", 0, 8), ("DD", 0, 8), ("DD", 8, 16), A.add)
-    tt(("FR", 0, 32), ("FL", 0, 32), ("RKD", 0, 32), A.mult)
-    ts2(("LC", 0, 8), ("MM", 0, 8), 256.0 * 128 - 127.5, 1.0 / 256.0, A.add, A.mult)
-    ts(("COL", 0, 8), ("MM", 0, 8), 255, A.bitwise_and)
+    ts(("LC", 0, 8), ("MM", 0, 8), 128.0, A.add)
     V4, L4 = window("V4", 0, 128), window("L4", 0, 128)
     pick_columns(V4, window("Z", 0, 256 + ZC), ("LC", 0, 8))
     mate = rank ^ 4
     exchange(mate, L4, V4, "arr3")
     arrive(L4, "arr3")
-    tt(("CD", 0, 8), ("COL", 0, 8), ("DG", 0, 8), A.mult)
-    total_of(("IDO", 0, 1), ("FR", 0, 32))
-    total_of(("IDO", 1, 2), ("CD", 0, 8))
+    for i in (0, 1):
+        total_of(("IDR", i, i + 1), ("IDN", i, 6, 2), A.max)
+    tt(("IDO", 0, 2), ("IDM", 0, 2), ("IDR", 0, 2), A.max)
     send(mate, ("IDA", 0, 2), ("IDO", 0, 2), "num3")
     arrive([("IDA", 0, 2)], "num3")
     for o in range(O):

@@ -27,32 +27,43 @@ SCRATCH.update(_sbuf(2, U16, "ZOFF"))
 SCRATCH.update(_sbuf(4, U16, "LU"))
 SCRATCH.update(_sbuf(4 * (N - 1), U16, "GOFF"))
 SCRATCH.update(_sbuf(4 * (N - 1), BF, "GO"))
-SCRATCH.update(_sbuf(1, I32, "PIDX"))
+SCRATCH.update(_sbuf(2, I32, "PIDX"))
 SCRATCH.update(_sbuf(3, I32, "PI"))
 SCRATCH.update(_sbuf(3, F32, "PF SA"))
-SCRATCH.update(_sbuf(1, F32, "MF1 SC0 SC SCB SCS PS NEG PG"))
+SCRATCH.update(_sbuf(1, F32, "MF1 SC0 SC SCB SCS PS NEG PA"))
 SCRATCH.update(_sbuf(2, F32, "SCO C2"))
-SCRATCH.update(_sbuf(2, BF, "RQ SH IDM IDR IDO IDA"))
-SCRATCH.update(_sbuf(8, BF, "T1 T2 T3 IDN MM"))
+SCRATCH.update(_sbuf(2, BF, "RQ SH IDM"))
+SCRATCH.update(_sbuf(4, F32, "IDO IDA"))
+SCRATCH.update(_sbuf(8, BF, "T1 T2 T3 IDN IDR IDC RK MM"))
 SCRATCH.update(_sbuf(16, F32, "SCR"))
 SCRATCH.update(_sbuf(16, BF, "DD"))
 SCRATCH.update(_sbuf(32, BF, "LV4 DT"))
 SCRATCH.update(_sbuf(32, F32, "IDB KC3"))
-SCRATCH.update(_sbuf(4, F32, "P2 P3 K0 K1 K128"))
+SCRATCH.update(_sbuf(4, F32, "P2"))
+SCRATCH.update(_sbuf(2, F32, "K0 C2P PLR"))
+SCRATCH.update(_sbuf(2, BF, "P3 RR"))
+SCRATCH.update(_sbuf(8, BF, "U1 U2"))
+SCRATCH.update(_sbuf(8, U16, "LE"))
 SCRATCH.update(_sbuf(64, BF, "JC JC0"))
-SCRATCH.update(_sbuf(256, BF, "J256 TR E1 E2"))
+SCRATCH.update(_sbuf(256, BF, "J256 TR TE"))
+SCRATCH.update(_sbuf(512, BF, "E1"))
 SCRATCH.update(_sbuf(384, BF, "MD"))
-SCRATCH.update(_sbuf(128, BF, "COLR TMOD HOLD HE HB BASE G FX FH KCB BXG GFX GH VAL EH"))
-SCRATCH.update(_sbuf(3 * OTH, BF, "CM"))
-SCRATCH.update(_sbuf(480, BF, "CA CS"))
+SCRATCH.update(_sbuf(128 + ZC, BF, "COLR"))
+SCRATCH.update(_sbuf(128, BF, "TMOD HOLD HE HB BASE G FX FH VAL E2"))
+SCRATCH.update(_sbuf(4 * OTH, BF, "CM"))
+SCRATCH.update(_sbuf(896, BF, "CS"))
+SCRATCH.update(_sbuf(2, U16, "JOFF LK"))
+SCRATCH.update(_sbuf(4, F32, "SU1 SU2 ST"))
+SCRATCH.update(_sbuf(32, F32, "JS"))
+SCRATCH.update(_sbuf(2, F32, "PG"))
 SCRATCH.update(_sbuf(OTH, F32, "EX0 EX"))
-SCRATCH.update(_sbuf(OTH + 1, F32, "TS"))
-SCRATCH.update(_sbuf(128, F32, "ST SW IDT"))
-SCRATCH.update(_sbuf(256, F32, "SF YB"))
+SCRATCH.update(_sbuf(OTH + 2, F32, "TS"))
+SCRATCH.update(_sbuf(128, F32, "SR SW IDT"))
+SCRATCH.update(_sbuf(256, F32, "SF SI YB"))
 PSUM_NAMES = ["BS0", "BS1", "BG0", "BG1", "BSG", "BB", "BY0", "BY1"]
 SCRATCH.update({n: ("psum", [128, 512], F32) for n in PSUM_NAMES})
 SEMAPHORES = ["v", "s", "t", "gc", "du", "dx0", "dx1", "dw0", "dw1", "dy", "did", "loc",
-              "arr1", "arr2", "arr3", "sca", "scb", "num1", "num2", "num3"]
+              "arr1", "arr2", "ars2", "arr3", "sca", "scb", "scc", "num1", "num2", "num3"]
 
 
 def rank_program(g, core, T, topo):
@@ -226,39 +237,34 @@ def rank_program(g, core, T, topo):
     fill(("UT", 8, 512), 0.0)
     fill(("XT", 1024, 1024 + 4 * ZC), 0.0)
     fill(("UOFF", 0, 8), 0)
+    fill(("ZOFF", 0, 2), 256)
     best = 256 if high else 0
-    fill(("MD", 0, 384), 1.0)
-    fill(("INV", best, best + 256), 0.0)
-    iota(("PIDX", 0, 1), [[0, 1]], 0, 1)
-    iota(("TMOD", 0, 128), [[0, 8], [1, 16]], 0, 0)
+    act(("MD", 0, 384), ("UT", 128, 512), F.Identity, 1.0)
+    scopy(("INV", best, best + 256), ("UT", 256, 512))
+    scopy(("SI", best // 2, best // 2 + 128), ("UT", 384, 512))
+    iota(("PIDX", 0, 2), [[128, 2]], 0, 1)
+    iota(("TMOD", 0, 32), [[0, 2], [1, 16]], 0, 0)
+    iota(("GO", 0, 4 * (N - 1)), [[1, 2 * (N - 1)], [0, 2]], 0, 0)
     diag = ("MD", 128, 256)
     do("g", lambda: g.affine_select(ap(diag), ap(diag), [[-1, 128]], A.not_equal, -1.0, 0, 1), [diag], [diag])
     iota(("C2", 0, 2), [[16, 2]], (127 if high else 128) - ROUND, 0)
     iota(("JC0", 0, 64), [[128, 2], [0, 2], [1, 16]], 0, 0)
-    iota(("GO", 0, 4 * (N - 1)), [[1, 2 * (N - 1)], [0, 2]], 0, 0)
-    iota(("K0", 0, 4), [[-32 if high else 32, 4]], 128 if high else 1, 0)
-    sign = -1 if upper else 1
-    iota(("J256", 0, 256), [[1, 256]], 1, 0)
-    for i, bits in enumerate((15, 31, 112)):
+    for i, bits in enumerate((15, 112)):
         ts(("PI", i, i + 1), ("PIDX", 0, 1), bits, A.bitwise_and)
-    copy(("PF", 0, 3), ("PI", 0, 3))
-    MF, PM, P16 = ("PF", 0, 1), ("PF", 1, 2), ("PF", 2, 3)
+    copy(("JOFF", 0, 2), ("PIDX", 0, 2))
+    copy(("PF", 0, 2), ("PI", 0, 2))
+    MF, P16 = ("PF", 0, 1), ("PF", 1, 2)
     act(("MF1", 0, 1), MF, F.Identity, 1.0)
-    act(("PS", 0, 1), PM, F.Identity, 0.0, -1.0 if high else 1.0)
-    act(("JC", 0, 64), ("JC0", 0, 64), F.Identity, P16)
-    ts(("HOLD", 0, 128), ("TMOD", 0, 128), MF, A.is_gt)
+    ts(("HOLD", 0, 32), ("TMOD", 0, 32), MF, A.is_gt)
     ts2(("SC0", 0, 1), MF, 15.0, 255.0 / 256.0, A.is_equal, A.mult)
-    ts2(("HE", 0, 128), ("TMOD", 0, 128), ("MF1", 0, 1), 255.0, A.is_equal, A.mult)
-    tt(("HB", 0, 128), ("HOLD", 0, 128), ("HE", 0, 128), A.add)
-    ts(("SC", 0, 1), ("SC0", 0, 1), 1.0 / 256.0, A.add)
-    ts2(("SCB", 0, 1), ("SC0", 0, 1), 1.0 / 256.0, 128.0, A.add, A.mult)
-    ts2(("SCS", 0, 1), ("SC0", 0, 1), 1.0 / 256.0, float(sign), A.add, A.mult)
+    copy(("GOFF", 0, 4 * (N - 1)), ("GO", 0, 4 * (N - 1)))
 
     U0, U = (("UQ0", 0, 128), ("US0", 0, 128)), (("UQ", 0, 128), ("US", 0, 128))
     quant(*U0, ("UT", 0, 512))
     quant(("XQ", 0, 128), ("XS", 0, 128), ("XT", 0, 512))
     pick_columns(U, U0, ("UOFF", 0, 8))
     quant(("XQ", 128, 256 + ZC), ("XS", 128, 256 + ZC), ("XT", 512, 1024 + 4 * ZC))
+    ts2(("HE", 0, 32), ("TMOD", 0, 32), ("MF1", 0, 1), 255.0, A.is_equal, A.mult)
 
     def equal(h, part):
         b = 256 * h + 128 * part
@@ -283,8 +289,11 @@ def rank_program(g, core, T, topo):
     near = [rank ^ d for d in (1, 2, 3)]
     spread(near, [("SCR", 2 * i, 2 * i + 2) for i in [(r4 - m - 1) % 4 if far else r4 - (r4 > m) for m in near]], ("SCO", 0, 2), "sca")
     arrive([("SCR", 0, 6)], "sca")
-    spread([rank ^ d for d in (4, 5, 6, 7)], [("SCR", 6 + 2 * r4, 8 + 2 * r4)] * 4, ("SCO", 0, 2), "scb")
-    arrive([("SCR", 6, 14)], "scb")
+    for ds, sem in (((4, 5), "scb"), ((6, 7), "scc")):
+        spread([rank ^ d for d in ds], [("SCR", 2 * d - 2, 2 * d) for d in ds], ("SCO", 0, 2), sem)
+        arrive([("SCR", 2 * ds[0] - 2, 2 * ds[-1])], sem)
+    iota(("K0", 0, 1), [[0, 1]], 2 * OTH if far else 0, 0)
+    iota(("C2P", 0, 2), [[16, 2]], (127 if high else 0) - ROUND, -1 if high else 1)
 
     for h, part in ((1, 0), (0, 1), (1, 1)):
         equal(h, part)
@@ -296,136 +305,156 @@ def rank_program(g, core, T, topo):
              0.0 if h else ("SA", 2, 3), A.mult, A.add)
     for h in (0, 1):
         ts2(("SH", h, h + 1), ("LS", 256 * h + 255, 256 * h + 256), ("SA", h, h + 1), 0.5 if high else -0.5, A.add, A.mult)
+    ts(("JC", 0, 64), ("JC0", 0, 64), P16, A.add)
+    tt(("HB", 0, 32), ("HOLD", 0, 32), ("HE", 0, 32), A.add)
+    spick(("JS", 0, 32), ("SF", 0, 256), ("JOFF", 0, 2))
+    act(("SCB", 0, 1), ("SC0", 0, 1), F.Identity, 0.5, 128.0)
     ts(("RQ", 0, 2), ("SH", 0, 2), (127.0 if high else 128.0) - 7.5 + ROUND, A.add)
+    ts(("LK", 0, 2), ("SH", 0, 2), 127.0 if high else 128.0, A.add)
     for h in (0, 1):
         ts2(("LU", 2 * h, 2 * h + 2), ("C2", 0, 2), ("RQ", h, h + 1), ("SH", h, h + 1), A.add, A.add)
+    vput(("SI", 0, 256), ("LK", 0, 2), ("JS", 0, 32))
     vput(("INV", 0, 512), ("LU", 0, 4), ("JC", 0, 64))
-    copy(("GOFF", 0, 4 * (N - 1)), ("GO", 0, 4 * (N - 1)))
+    turn(("SR", 0, 128), ("SI", best // 2, best // 2 + 128))
     a, z = (0, 128) if high else (128, 0)
     turn(("TR", 0, 256), ("INV", best, best + 256))
+    tt(("SU1", 0, 4), ("SR", 0, 128, 32), ("SR", 16, 128, 32), A.add)
     tt(("T1", 0, 8), ("TR", 0, 256, 32), ("TR", 16, 256, 32), A.add)
+    tt(quad("SU2", 0, 4, 0, 64), quad("SU1", 0, 4, 0, 64), quad("SU1", 0, 4, 64, 64), A.add)
     tt(quad("T2", 0, 8, 0, 64), quad("T1", 0, 8, 0, 64), quad("T1", 0, 8, 64, 64), A.add)
-    for p in (0, 32):
-        tt(quad("T3", 0, 8, p), quad("T2", 0, 8, 0), quad("T2", 0, 8, 32), A.add)
+    for name, src, n, p in (("ST", "SU2", 4, 0), ("ST", "SU2", 4, 32), ("T3", "T2", 8, 0), ("T3", "T2", 8, 32),
+                            ("ST", "SU2", 4, 64), ("ST", "SU2", 4, 96)):
+        tt(quad(name, 0, n, p), quad(src, 0, n, 0), quad(src, 0, n, 32), A.add)
     for p in (0, 64):
         copy(quad("NN", 0, 8, p, 64), quad("T3", 0, 8, 0, 64))
-    act(("K1", 0, 4), ("K0", 0, 4), F.Identity, ("PS", 0, 1))
-    act(("BASE", 0, 128), ("J256", 0, 128), F.Identity, 1.0, 1.0 / 128.0)
-    act(("E1", 0, 128), ("J256", 0, 128), F.Identity, 1.0, 0.0)
-    act(("VAL", 0, 128), ("J256", 0, 128), F.Identity, 130.0 if upper else float(ZC), float(sign))
-    for c in range(4):
-        act(("KCB", 32 * c, 32 * c + 32), ("J256", 0, 32), F.Identity, ("K1", c, c + 1), 0.0)
-    act(("K128", 0, 4), ("K1", 0, 4), F.Identity, 128.0)
-    if far:
-        act(("KC3", 0, 32), ("KCB", 96, 128), F.Identity, 4.0 * OTH)
+    scopy(("E1", 0, 256), ("UT", 256, 512))
+    b = 128 if upper else 0
+    scopy(("COLR", b, b + ZC), ("UT", 256, 256 + ZC))
+    act(("VAL", 0, 32), ("JC", 0, 32), F.Identity, -128.0 if upper else float(ZC))
+    for n in (32, 64):
+        scopy(("HB", n, 2 * n), ("HB", 0, n))
     own, got = window("W1", a, a + 128), window("W1", z, z + 128)
     NEAR, MID = 192, 320
     cut = 64 * (3 - r4 if far else r4)
-    split = 64 if cut == 64 else 128
-    vpick(("EX0", 0, NEAR), ("SCR", 0, 6), ("GOFF", 0, NEAR // 16))
-    spick(("SW", 0, 128), ("SF", 0, 256), ("NN", 0, 8))
+    pick_columns(window("Z", 128, 128 + ZC), window("X", 0, 256 + ZC), ("ZOFF", 0, 1))
+    spick(("EX0", 0, NEAR), ("SCR", 0, 6), ("GOFF", 0, NEAR // 16))
     pick_columns(own, window("X", 0, 256), ("NN", 0, 8))
-    turn(("EX", 0, split), ("EX0", 0, split))
-    turn(("ST", 0, 128), ("SW", 0, 128))
-    turn(("EX", split, NEAR), ("EX0", split, NEAR))
+    split = 64 if cut == 64 else 128
+    for b, e in ((0, split), (split, NEAR)):
+        turn(("EX", b, e), ("EX0", b, e))
 
     mate = rank ^ 1
     exchange(mate, own, own, "arr1")
     arrive(got, "arr1")
+    iota(("J256", 0, 256), [[N, 256]], N, 0)
+    if r4 < 3:
+        iota(("RK", 0, 3 - r4), [[1, 3 - r4]], rank + 1, 0)
+    if r4:
+        iota(("RK", 3 - r4, 3), [[1, r4]], far, 0)
     for o in range(O):
         hold("y", [("XT", 0, 512)], [])
         load("y", ("WT", 512 * o, 512 * o + 512), T.w[:, 512 * o:512 * o + 512], "dw%d" % o)
-    for b, e in ((NEAR, MID), (MID, OTH)):
-        spick(("EX0", b, e), ("SCR", 0, 14), ("GOFF", b // 16, e // 16))
+    spick(("EX0", NEAR, MID), ("SCR", 0, 10), ("GOFF", NEAR // 16, MID // 16))
     ops = (A.is_gt, A.is_ge) if far else (A.is_ge, A.is_gt)
 
-    def beats(c, b, e):
-        s, o = ("ST", 32 * c, 32 * c + 1), OTH * c
+    def beats(c, b, e, shift=0):
+        s, o = ("ST", c, c + 1), OTH * c + shift
         if b < cut:
             ts(("CM", o + b, o + min(e, cut)), ("EX", b, min(e, cut)), s, ops[0])
         if max(b, cut) < e:
             ts(("CM", o + max(b, cut), o + e), ("EX", max(b, cut), e), s, ops[1])
 
-    def count(name, c, b, e, init=0.0):
-        m, end = (e - b) // 2, 160 * c + 160
-        o = OTH * c + b
-        scan((name, end - m, end), ("CM", o, o + m), ("CM", o + m, o + 2 * m), init, A.add, A.add)
+    def count(c, n, init=0.0):
+        m, end, o = n // 2, 224 * c + 224, OTH * c
+        scan(("CS", end - m, end), ("CM", o, o + m), ("CM", o + m, o + n), init, A.add, A.add)
 
     way = 1.0 if far else -1.0
-    act(("TS", 0, NEAR), ("EX", 0, NEAR), F.Sign, ("ST", 96, 97), -1.0)
+
+    def signs(b, e, shift=0):
+        act(("TS", b + shift, e + shift), ("EX", b, e), F.Sign, ("ST", 3, 4), -1.0)
+
+    signs(0, NEAR)
+    spick(("EX0", MID, OTH), ("SCR", 0, 14), ("GOFF", MID // 16, OTH // 16))
     if cut:
-        act(("TS", 0, cut), ("TS", 0, cut), F.Sign, way, 1.0, ("TS", OTH, OTH + 1))
+        act(("TS", 0, cut), ("TS", 0, cut), F.Sign, way, 1.0, ("TS", MID, MID + 1))
     beats(0, 0, split)
     beats(0, split, NEAR)
-    for c in (1, 2):
-        beats(c, 0, NEAR)
-    for b, e in ((NEAR, MID), (MID, OTH)):
-        turn(("EX", b, e), ("EX0", b, e))
-    for c in range(3):
-        count("CA", c, 0, NEAR)
-    act(("TS", NEAR, OTH), ("EX", NEAR, OTH), F.Sign, ("ST", 96, 97), -1.0)
-    rest = ("TS", cut, OTH + 1 if cut else OTH)
+    beats(1, 0, NEAR)
+    turn(("EX", NEAR, MID), ("EX0", NEAR, MID))
+    signs(NEAR, MID)
+    spick(("SW", 0, 128), ("SF", 0, 256), ("NN", 0, 8))
+    rest = ("TS", cut, MID + 1 if cut else MID)
+    act(rest, rest, F.Relu, 0.0, way, ("PG", 1, 2))
+    beats(2, 0, NEAR)
+    for c in (0, 1):
+        beats(c, NEAR, MID)
+    turn(("EX", MID, OTH), ("EX0", MID, OTH))
+    signs(MID, OTH, 1)
+    rest = ("TS", MID + 1, OTH + 1)
     act(rest, rest, F.Relu, 0.0, way, ("PG", 0, 1))
-    spick(("COLR", 0, 128), ("J256", 0, 256), ("NN", 0, 8))
-    act(("E2", 0, 128), ("J256", 0, 128), F.Identity, 0.0, 0.0)
+    act(("PLR", 0, 1), ("C2P", 0, 1), F.Identity, 2 * ROUND - 7.5)
+    act(("BASE", 0, 128), ("J256", 0, 128), F.Identity, 1.0, 1.0 / (128.0 * N))
+    b = 0 if upper else ZC
+    spick(("COLR", b, b + 128), ("J256", 0, 256), ("NN", 0, 8))
+    beats(2, NEAR, MID)
     for c in range(3):
-        beats(c, NEAR, OTH)
+        beats(c, MID, OTH)
     for c in range(3):
-        count("CS", c, NEAR, OTH, ("CA", 160 * c + 159, 160 * c + 160))
+        count(c, OTH)
+    op = A.subtract if far else A.add
+    ts2(quad("PA", 0, 1, 0, 64), quad("K0", 0, 1, 0, 64), quad("PG", 1, 2, 0, 64), quad("PG", 1, 2, 64, 64), op, op)
     mm(("BB", 0, 128), *U, *got)
-    tt(quad("P2", 3, 4, 0, 64), quad("PG", 0, 1, 0, 64), quad("PG", 0, 1, 64, 64), A.add)
-    tt(quad("P2", 0, 3, 0, 64), quad("CS", 159, 480, 0, 64, 160), quad("CS", 159, 480, 64, 64, 160), A.add)
-    for p in (0, 32):
-        tt(quad("P3", 0, 4, p), quad("P2", 0, 4, 0), quad("P2", 0, 4, 32), A.add)
-    tt(("G", 0, 128), ("BB", 0, 128), ("SW", 0, 128), A.is_lt if high else A.is_gt)
+    tt(quad("P2", 0, 3, 0, 64), quad("CS", 223, 672, 0, 64, 224), quad("CS", 223, 672, 64, 64, 224), A.add)
+    ts2(quad("P2", 3, 4, 0, 64), quad("PA", 0, 1, 0, 64), quad("PG", 0, 1, 0, 64), quad("PG", 0, 1, 64, 64), op, op)
     for c in range(4):
-        b = (32 * c, 32 * c + 32, 0, 64)
-        first, op = (quad("KC3", 0, 32, 0, 64), A.subtract) if far and c == 3 else (quad("KCB", *b), A.add)
-        ts2(quad("BXG", *b), first, quad("P3", c, c + 1, 0, 64), quad("K128", c, c + 1, 0, 64), op, A.min)
+        ts2(quad("P3", 0, 1, 32 * c), quad("P2", c, c + 1, 0), quad("P2", c, c + 1, 32), 128.0, A.add, A.min)
+    tt(("G", 0, 128), ("BB", 0, 128), ("SW", 0, 128), A.is_lt if high else A.is_gt)
+    ts(("RR", 0, 1), ("P3", 0, 1), ("PLR", 0, 1), A.add)
     scan(("FX", 0, 128), ("BASE", 0, 128), ("G", 0, 128), 0.0, A.max, A.subtract)
-    turn(quad("GFX", 0, 128, 0, 64), quad("BXG", 0, 128, 0, 64))
+    ts2(("LUG", 0, 2), ("C2P", 0, 2), ("RR", 0, 1), ("P3", 0, 1), A.add, A.add)
     hold16(("FH", 0, 128), ("FX", 0, 128))
-    scan(quad("GH", 0, 128, 0, 64), quad("HB", 0, 128, 0, 64), quad("GFX", 0, 128, 0, 64), 0.0, A.mult, A.max)
+    vput(("E1", 0, 512), ("LUG", 0, 2), ("VAL", 0, 32))
     take16(("LOF", 0, 8), ("FH", 0, 128), 1.0, "SCB")
-    for p in (0, 64):
-        ts2(quad("LUG", 0, 8, p, 64), quad("GH", 15, 128, 0, 64, 16), quad("SC", 0, 1, 0, 64), 1.0, A.mult, A.subtract)
+    turn(("TE", 0, 256), ("E1", 0, 256))
     z2 = 0 if upper else 128 + ZC
     S2 = window("Z", z2, z2 + 128)
     L2 = window("Z", 128 + ZC - z2, 256 + ZC - z2)
     pick_columns(S2, window("W1", 0, 256), ("LOF", 0, 8))
     send(rank ^ 2, S2[0], S2[0], "arr2", codes=True)
-    vput(("E1", 0, 256), ("LUG", 0, 8), ("VAL", 0, 128))
-    fill(("ZOFF", 0, 2), 256)
-    hold16(("EH", 0, 128), ("E1", 0, 128))
+    arrive([L2[0]], "arr2")
+    tt(("U1", 0, 8), ("TE", 0, 256, 32), ("TE", 16, 256, 32), A.add)
+    fill(("IDB", 0, 32), 0.0)
+    tt(quad("U2", 0, 8, 0, 64), quad("U1", 0, 8, 0, 64), quad("U1", 0, 8, 64, 64), A.add)
     mine = ("LV4", 8 * r4, 8 * r4 + 8)
-    take16(mine, ("EH", 0, 128), float(sign), "SCS")
+    for p in (0, 32, 64, 96):
+        tt(quad(*mine, p), quad("U2", 0, 8, 0), quad("U2", 0, 8, 32), A.add)
     spread(near, [mine] * 3, mine, "num1")
     arrive([("LV4", 8 * (m & 3), 8 * (m & 3) + 8) for m in near], "num1")
-    send(rank ^ 2, S2[1], S2[1], "arr2")
-    arrive(L2, "arr2")
-    vput(("E2", 0, 256), ("LUG", 0, 8), ("COLR", 0, 128))
-    pick_columns(window("Z", 128, 128 + ZC), window("X", 0, 256 + ZC), ("ZOFF", 0, 1))
+    send(rank ^ 2, S2[1], S2[1], "ars2")
+    arrive([L2[1]], "ars2")
+    ts(("LE", 0, 8), mine, 128.0 if upper else 0.0, A.add)
+    vpick(("E2", 0, 128), ("COLR", 0, 128 + ZC), ("LE", 0, 8))
     for a in range(4):
         turn(quad("DT", 0, 32, 32 * a), quad("E2", 32 * a, 32 * a + 32, 32 * a))
-    ts2(("IDM", 0, 1), ("DT", 0, 1), 0.0, float(rank), A.is_gt, A.mult)
-    ts2(("IDM", 1, 2), ("DT", 0, 1), 1.0, 0.0, A.subtract, A.max)
-    spread(near, [("IDN", 2 * d, 2 * d + 2) for d in range(3)], ("IDM", 0, 2), "num2")
-    arrive([("IDN", 0, 6)], "num2")
-    for o in range(O):
-        quant(("WQ", 128 * o, 128 * o + 128), ("WS", 128 * o, 128 * o + 128), ("WT", 512 * o, 512 * o + 512))
-    fill(("IDB", 0, 32), 0.0)
+    spread(near, [("IDN", i, i + 1) for i in [(rank - m - 1) % 4 for m in near]], ("DT", 0, 1), "num2")
+    arrive([("IDN", 0, 3)], "num2")
+    ts(("IDM", 0, 1), ("DT", 0, 1), float(rank), A.min)
     tt(("DD", 0, 16), ("LV4", 0, 16), ("LV4", 16, 32), A.add)
+    quant(*window("W", 0, 128), ("WT", 0, 512))
     tt(("MM", 0, 8), ("DD", 0, 8), ("DD", 8, 16), A.add)
+    quant(*window("W", 128, 256), ("WT", 512, 1024))
     ts(("LC", 0, 8), ("MM", 0, 8), 128.0, A.add)
     V4, L4 = window("V4", 0, 128), window("L4", 0, 128)
     pick_columns(V4, window("Z", 0, 256 + ZC), ("LC", 0, 8))
     mate = rank ^ 4
     exchange(mate, L4, V4, "arr3")
     arrive(L4, "arr3")
-    for i in (0, 1):
-        total_of(("IDR", i, i + 1), ("IDN", i, 6, 2), A.max)
-    tt(("IDO", 0, 2), ("IDM", 0, 2), ("IDR", 0, 2), A.max)
-    send(mate, ("IDA", 0, 2), ("IDO", 0, 2), "num3")
+    got3 = ("IDN", 0, 3)
+    tt(("IDR", 0, 3), got3, ("RK", 0, 3), A.min)
+    scan(("IDC", 0, 3), got3, got3, ("DT", 0, 1), A.max, A.max)
+    scan(("IDO", 0, 3), ("IDR", 0, 3), ("IDR", 0, 3), ("IDM", 0, 1), A.max, A.max)
+    ts2(("IDO", 3, 4), ("IDC", 2, 3), 1.0 / N, 0.5, A.mult, A.subtract)
+    send(mate, ("IDA", 0, 2), ("IDO", 2, 4), "num3")
     arrive([("IDA", 0, 2)], "num3")
     for o in range(O):
         mm(("BY%d" % o, 0, 128), *window("W", 128 * o, 128 * o + 128), *V4, True, False)
@@ -434,10 +463,10 @@ def rank_program(g, core, T, topo):
     scopy(("YB", 128, 256), ("BY1", 0, 128))
     copy(("YB", 0, 128), ("BY0", 0, 128))
     do("y", lambda: g.sync.dma_start(T.y[:, :], ap(("YB", 0, 256))), [], [("YB", 0, 256)], "dy", 16)
-    tt(("IDB", 0, 2), ("IDO", 0, 2), ("IDA", 0, 2), A.add)
-    for a in range(4):
-        turn(quad("IDT", 32 * a, 32 * a + 32, 0), quad("IDB", 0, 32, 32 * a))
-    do("s", lambda: g.scalar.dma_start(T.id[:, :], T.IDT[0:2, 0:128]), [], [("IDT", 0, 128)], "did", 16)
+    tt(("IDB", 0, 2), ("IDO", 2, 4), ("IDA", 0, 2), A.add)
+    turn(("IDT", 0, 32), ("IDB", 0, 32))
+    for row in (0, 1):
+        do("s", lambda: g.scalar.dma_start(T.id[row, :], T.IDT[row:128:32, 0:32]), [], [("IDT", 0, 32)], "did", 16)
     late = ("t", "v", "s", "did", "dy")
     for sem in sorted(x for x in total if x not in late) + list(late):
         if known["g"].get(sem, 0) < total[sem]:

from concourse.bass import DstId, RemoteDMATransfer
from concourse.mybir import dt, AluOpType, ActivationFunctionType, AxisListType

N, T_COLS, K, O = 8, 256, 128, 2
BF, F32, U16, I32, CODE, U8 = "bfloat16", "float32", "uint16", "int32", "float8_e4m3fn_x4", "uint8"
OTH = 64 * (N - 1)
ZC = 16
ROUND = 2064


def _sbuf(cols, dtype, names):
    return {n: ("sbuf", [128, cols], dtype) for n in names.split()}


SCRATCH = {}
SCRATCH.update(_sbuf(512, BF, "UT INV EQ LS SG"))
SCRATCH.update(_sbuf(1024 + 4 * ZC, BF, "XT"))
SCRATCH.update(_sbuf(1024, BF, "WT"))
SCRATCH.update(_sbuf(128, CODE, "UQ0 UQ V4Q L4Q"))
SCRATCH.update(_sbuf(128, U8, "US0 US V4S L4S"))
SCRATCH.update(_sbuf(256, CODE, "WQ W1Q"))
SCRATCH.update(_sbuf(256, U8, "WS W1S"))
SCRATCH.update(_sbuf(256 + ZC, CODE, "XQ ZQ"))
SCRATCH.update(_sbuf(256 + ZC, U8, "XS ZS"))
SCRATCH.update(_sbuf(8, U16, "UOFF NN LOF LUG LC"))
SCRATCH.update(_sbuf(2, U16, "ZOFF"))
SCRATCH.update(_sbuf(4, U16, "LU"))
SCRATCH.update(_sbuf(4 * (N - 1), U16, "GOFF"))
SCRATCH.update(_sbuf(4 * (N - 1), BF, "GO"))
SCRATCH.update(_sbuf(2, I32, "PIDX"))
SCRATCH.update(_sbuf(3, I32, "PI"))
SCRATCH.update(_sbuf(3, F32, "PF SA"))
SCRATCH.update(_sbuf(1, F32, "MF1 SC0 SC SCB SCS PS NEG PA"))
SCRATCH.update(_sbuf(2, F32, "SCO C2"))
SCRATCH.update(_sbuf(2, BF, "RQ SH IDM"))
SCRATCH.update(_sbuf(4, F32, "IDO IDA"))
SCRATCH.update(_sbuf(8, BF, "T1 T2 T3 IDN IDR IDC RK MM"))
SCRATCH.update(_sbuf(16, F32, "SCR"))
SCRATCH.update(_sbuf(16, BF, "DD"))
SCRATCH.update(_sbuf(32, BF, "LV4 DT"))
SCRATCH.update(_sbuf(32, F32, "IDB KC3"))
SCRATCH.update(_sbuf(4, F32, "P2"))
SCRATCH.update(_sbuf(2, F32, "K0 C2P PLR"))
SCRATCH.update(_sbuf(2, BF, "P3 RR"))
SCRATCH.update(_sbuf(8, BF, "U1 U2"))
SCRATCH.update(_sbuf(8, U16, "LE"))
SCRATCH.update(_sbuf(64, BF, "JC JC0"))
SCRATCH.update(_sbuf(256, BF, "J256 TR TE"))
SCRATCH.update(_sbuf(512, BF, "E1"))
SCRATCH.update(_sbuf(384, BF, "MD"))
SCRATCH.update(_sbuf(128 + ZC, BF, "COLR"))
SCRATCH.update(_sbuf(128, BF, "TMOD HOLD HE HB BASE G FX FH VAL E2"))
SCRATCH.update(_sbuf(4 * OTH, BF, "CM"))
SCRATCH.update(_sbuf(896, BF, "CS"))
SCRATCH.update(_sbuf(2, U16, "JOFF LK"))
SCRATCH.update(_sbuf(4, F32, "SU1 SU2 ST"))
SCRATCH.update(_sbuf(32, F32, "JS"))
SCRATCH.update(_sbuf(2, F32, "PG"))
SCRATCH.update(_sbuf(OTH, F32, "EX0 EX"))
SCRATCH.update(_sbuf(OTH + 2, F32, "TS"))
SCRATCH.update(_sbuf(128, F32, "SR SW IDT"))
SCRATCH.update(_sbuf(256, F32, "SF SI YB"))
PSUM_NAMES = ["BS0", "BS1", "BG0", "BG1", "BSG", "BB", "BY0", "BY1"]
SCRATCH.update({n: ("psum", [128, 512], F32) for n in PSUM_NAMES})
SEMAPHORES = ["v", "s", "t", "gc", "du", "dx0", "dx1", "dw0", "dw1", "dy", "did", "loc",
              "arr1", "arr2", "ars2", "arr3", "sca", "scb", "scc", "num1", "num2", "num3"]


def rank_program(g, core, T, topo):
    rank = T.rank_of(core)
    if rank is None:
        return
    A = AluOpType
    F = ActivationFunctionType
    engines = {"v": g.vector, "s": g.scalar, "t": g.tensor, "g": g, "y": g.sync}
    known = {q: {} for q in engines}
    total = {}
    hist = {}

    def parts(r):
        return (r[4], r[5]) if len(r) > 4 else (0, 128)

    def record(reads, writes, q, sem, val, clock):
        for rs, w in ((reads, False), (writes, True)):
            for r in rs:
                hist.setdefault(r[0], []).append((r[1], r[2]) + parts(r) + (w, q, sem, val, clock))

    def hold(q, reads, writes):
        need = {}
        for rs, w in ((reads, False), (writes, True)):
            for r in rs:
                psum = r[0] in PSUM_NAMES
                a, z = parts(r)
                for lo, hi, p0, p1, hw, hq, sem, val, clock in hist.get(r[0], []):
                    if not (psum or (lo < r[2] and r[1] < hi and p0 < z and a < p1)):
                        continue
                    if not (w or hw or (psum and hq != q)):
                        continue
                    if known[q].get(sem, 0) < val and (sem not in need or need[sem][0] < val):
                        need[sem] = (val, clock)
        for sem in sorted(need):
            val, clock = need[sem]
            if any(o != sem and need[o][1].get(sem, 0) >= val for o in need):
                continue
            engines[q].wait_ge(T.sem[sem], val)
        for sem in need:
            val, clock = need[sem]
            for s, x in list(clock.items()) + [(sem, val)]:
                known[q][s] = max(known[q].get(s, 0), x)

    def do(q, call, writes, reads, sem=None, inc=1):
        sem = sem or {"g": "gc"}.get(q, q)
        hold(q, reads, writes)
        call().then_inc(T.sem[sem], inc)
        total[sem] = total.get(sem, 0) + inc
        clock = dict(known[q])
        clock[sem] = total[sem]
        record(reads, writes, q, sem, total[sem], clock)

    def ap(r):
        if len(r) == 3:
            return T[r[0]][:, r[1]:r[2]]
        p, z = parts(r)
        return T[r[0]][p:z, r[1]:r[2]:r[3]]

    def quad(name, a, b, p, n=32, step=1):
        return (name, a, b, step, p, p + n)

    def words(r):
        return ap(r).bitcast(dt.uint32)

    def ts2(out, in0, s, s2, op0, op1):
        cols = [x for x in (s, s2) if isinstance(x, tuple)]
        a, b = [ap(x) if isinstance(x, tuple) else x for x in (s, s2)]
        last = () if op1 is None else (op1,)
        do("v", lambda: g.vector.tensor_scalar(ap(out), ap(in0), a, b, op0, *last), [out], [in0] + cols)

    def ts(out, in0, s, op):
        ts2(out, in0, s, None, op, None)

    def tt(out, a, b, op):
        do("v", lambda: g.vector.tensor_tensor(ap(out), ap(a), ap(b), op), [out], [a, b])

    def scan(out, a, b, init, op0, op1):
        cols = [init] if isinstance(init, tuple) else []
        do("v", lambda: g.vector.tensor_tensor_scan(ap(out), ap(a), ap(b), ap(init) if cols else init, op0, op1), [out], [a, b] + cols)

    def total_of(out, a, op=A.add):
        do("v", lambda: g.vector.tensor_reduce(ap(out), ap(a), AxisListType.X, op), [out], [a])

    def turn(out, a):
        do("v", lambda: g.vector.transpose(ap(out), ap(a)), [out], [a])

    def copy(out, a):
        do("v", lambda: g.vector.tensor_copy(ap(out), ap(a)), [out], [a])

    def scopy(out, a):
        do("s", lambda: g.scalar.activation(ap(out), ap(a), F.Copy), [out], [a])

    def act(out, a, func, bias=0.0, scale=1.0, sums=None):
        cols = [bias] if isinstance(bias, tuple) else []
        do("s", lambda: g.scalar.activation(ap(out), ap(a), func, bias=ap(bias) if cols else bias, scale=scale,
                                            accum_out=ap(sums) if sums else None), [out] + ([sums] if sums else []), [a] + cols)

    def vpick(out, win, off):
        do("v", lambda: g.vector.tensor_copy(ap(out), ap(win).indirect(ap(off))), [out], [win, off])

    def vput(win, off, src):
        do("v", lambda: g.vector.tensor_copy(ap(win).indirect(ap(off)), ap(src)), [win], [off, src])

    def spick(out, win, off):
        do("s", lambda: g.scalar.activation(ap(out), ap(win).indirect(ap(off)), F.Copy), [out], [win, off])

    def pick_columns(out, win, off):
        do("v", lambda: g.vector.tensor_copy(words(out[0]), words(win[0]).indirect(ap(off))), [out[0]], [win[0], off])
        spick(out[1], win[1], off)

    def fill(out, x):
        do("v", lambda: g.vector.memset(ap(out), x), [out], [])

    def iota(out, pattern, base, cm):
        do("g", lambda: g.iota(ap(out), pattern, base, cm, allow_small_or_imprecise_dtypes=True), [out], [])

    def quant(q, s, t):
        do("v", lambda: g.vector.quantize_mx(ap(q), ap(s), ap(t)), [q, s], [t])

    def mm(out, wq, ws, xq, xs, start=True, stop=True):
        do("t", lambda: g.tensor.matmul_mx(ap(out), ap(wq), ap(ws), ap(xq), ap(xs), start, stop), [out], [wq, ws, xq, xs])

    def hold16(tmp, x):
        scan(tmp, ("HB", 0, 128), x, 0.0, A.mult, A.max)

    def take16(out, tmp, less, scale="SC"):
        ts2(out, (tmp[0], 15, 128, 16), (scale, 0, 1), less, A.mult, A.subtract)

    def load(q, out, src, sem):
        do(q, lambda: engines[q].dma_start(ap(out), src), [out], [], sem, 16)

    def sent(mate, rsem, copies=1):
        n = len(topo.engines(core, T.cores[mate]))
        total["loc"] = total.get("loc", 0) + n
        total[rsem] = total.get(rsem, 0) + n * copies

    def send(mate, out, src, rsem, codes=False):
        dst = T.cores[mate]
        hold("g", [src], [])
        rid, pid = topo.addr(dst, core)
        a, b = (ap(out).bitcast(dt.uint8), ap(src).bitcast(dt.uint8)) if codes else (ap(out), ap(src))
        g.remote_dma(a, b, T.sem[rsem], T.sem["loc"], pid, rid, topo.mask(core, dst))
        sent(mate, rsem)

    def spread(mates, outs, src, rsem):
        hold("g", [src], [])
        ids = [topo.addr(T.cores[m], core) for m in mates]
        g.remote_dma_fused([RemoteDMATransfer(
            dst_ids=[DstId(rid=rid, pnc=pid) for rid, pid in ids], dma_engine_mask=topo.mask(core, T.cores[mates[0]]),
            remote_sem=T.sem[rsem], src=ap(src), dsts=[ap(o) for o in outs])], local_sem=T.sem["loc"])
        sent(mates[0], rsem, len(mates))

    def arrive(regions, sem):
        record([], regions, "-", sem, total[sem], {sem: total[sem]})

    def exchange(mate, out, src, sem):
        send(mate, out[0], src[0], sem, codes=True)
        send(mate, out[1], src[1], sem)

    def window(name, a, b):
        return (name + "Q", a, b), (name + "S", a, b)

    high = rank & 1
    upper = rank & 2

    load("y", ("UT", 0, 8), T.u[:, 0:8], "du")
    load("s", ("XT", 0, 512), T.x[:, 0:512], "dx0")
    load("y", ("XT", 512, 1024), T.x[:, 512:1024], "dx1")

    fill(("UT", 8, 512), 0.0)
    fill(("XT", 1024, 1024 + 4 * ZC), 0.0)
    fill(("UOFF", 0, 8), 0)
    fill(("ZOFF", 0, 2), 256)
    best = 256 if high else 0
    act(("MD", 0, 384), ("UT", 128, 512), F.Identity, 1.0)
    scopy(("INV", best, best + 256), ("UT", 256, 512))
    scopy(("SI", best // 2, best // 2 + 128), ("UT", 384, 512))
    iota(("PIDX", 0, 2), [[128, 2]], 0, 1)
    iota(("TMOD", 0, 32), [[0, 2], [1, 16]], 0, 0)
    iota(("GO", 0, 4 * (N - 1)), [[1, 2 * (N - 1)], [0, 2]], 0, 0)
    diag = ("MD", 128, 256)
    do("g", lambda: g.affine_select(ap(diag), ap(diag), [[-1, 128]], A.not_equal, -1.0, 0, 1), [diag], [diag])
    iota(("C2", 0, 2), [[16, 2]], (127 if high else 128) - ROUND, 0)
    iota(("JC0", 0, 64), [[128, 2], [0, 2], [1, 16]], 0, 0)
    for i, bits in enumerate((15, 112)):
        ts(("PI", i, i + 1), ("PIDX", 0, 1), bits, A.bitwise_and)
    copy(("JOFF", 0, 2), ("PIDX", 0, 2))
    copy(("PF", 0, 2), ("PI", 0, 2))
    MF, P16 = ("PF", 0, 1), ("PF", 1, 2)
    act(("MF1", 0, 1), MF, F.Identity, 1.0)
    ts(("HOLD", 0, 32), ("TMOD", 0, 32), MF, A.is_gt)
    ts2(("SC0", 0, 1), MF, 15.0, 255.0 / 256.0, A.is_equal, A.mult)
    copy(("GOFF", 0, 4 * (N - 1)), ("GO", 0, 4 * (N - 1)))

    U0, U = (("UQ0", 0, 128), ("US0", 0, 128)), (("UQ", 0, 128), ("US", 0, 128))
    quant(*U0, ("UT", 0, 512))
    quant(("XQ", 0, 128), ("XS", 0, 128), ("XT", 0, 512))
    pick_columns(U, U0, ("UOFF", 0, 8))
    quant(("XQ", 128, 256 + ZC), ("XS", 128, 256 + ZC), ("XT", 512, 1024 + 4 * ZC))
    ts2(("HE", 0, 32), ("TMOD", 0, 32), ("MF1", 0, 1), 255.0, A.is_equal, A.mult)

    def equal(h, part):
        b = 256 * h + 128 * part
        if h:
            ts(("EQ", b, b + 128), ("BS%d" % part, 0, 128), ("BY1", 0, 1), A.is_equal)
        else:
            ts2(("EQ", b, b + 128), ("BS%d" % part, 0, 128), ("NEG", 0, 1), 0.0, A.add, A.is_equal)

    for h in (0, 1):
        x = window("X", 128 * h, 128 * h + 128)
        mm(("BY%d" % h, 0, 128), *x, *U0)
        if h == 0:
            act(("NEG", 0, 1), ("BY0", 0, 1), F.Identity, 0.0, -1.0)
        (copy if h else scopy)(("SCO", h, h + 1), ("BY%d" % h, 0, 1))
        for bank in (("BG1", "BS1") if h else ("BS0", "BG0")):
            mm((bank, 0, 128), *U, *x)
        if h == 0:
            equal(0, 0)
            act(("SG", 0, 128), ("BG0", 0, 128), F.Sign, ("NEG", 0, 1), 1.0, ("SA", 2, 3))
    mm(("BSG", 0, 256), *U, *window("X", 0, 256))
    r4, far = rank & 3, rank & 4
    near = [rank ^ d for d in (1, 2, 3)]
    spread(near, [("SCR", 2 * i, 2 * i + 2) for i in [(r4 - m - 1) % 4 if far else r4 - (r4 > m) for m in near]], ("SCO", 0, 2), "sca")
    arrive([("SCR", 0, 6)], "sca")
    for ds, sem in (((4, 5), "scb"), ((6, 7), "scc")):
        spread([rank ^ d for d in ds], [("SCR", 2 * d - 2, 2 * d) for d in ds], ("SCO", 0, 2), sem)
        arrive([("SCR", 2 * ds[0] - 2, 2 * ds[-1])], sem)
    iota(("K0", 0, 1), [[0, 1]], 2 * OTH if far else 0, 0)
    iota(("C2P", 0, 2), [[16, 2]], (127 if high else 0) - ROUND, -1 if high else 1)

    for h, part in ((1, 0), (0, 1), (1, 1)):
        equal(h, part)
    act(("SG", 128, 256), ("BG1", 0, 128), F.Sign, ("SCO", 0, 1), -1.0, ("SA", 0, 1))
    act(("SG", 256, 512), ("BSG", 0, 256), F.Sign, ("SCO", 1, 2), -1.0, ("SA", 1, 2))
    scopy(("SF", 0, 256), ("BSG", 0, 256))
    for h in (0, 1):
        scan(("LS", 256 * h, 256 * h + 256), ("MD", 128 - 128 * h, 384 - 128 * h), ("EQ", 256 * h, 256 * h + 256),
             0.0 if h else ("SA", 2, 3), A.mult, A.add)
    for h in (0, 1):
        ts2(("SH", h, h + 1), ("LS", 256 * h + 255, 256 * h + 256), ("SA", h, h + 1), 0.5 if high else -0.5, A.add, A.mult)
    ts(("JC", 0, 64), ("JC0", 0, 64), P16, A.add)
    tt(("HB", 0, 32), ("HOLD", 0, 32), ("HE", 0, 32), A.add)
    spick(("JS", 0, 32), ("SF", 0, 256), ("JOFF", 0, 2))
    act(("SCB", 0, 1), ("SC0", 0, 1), F.Identity, 0.5, 128.0)
    ts(("RQ", 0, 2), ("SH", 0, 2), (127.0 if high else 128.0) - 7.5 + ROUND, A.add)
    ts(("LK", 0, 2), ("SH", 0, 2), 127.0 if high else 128.0, A.add)
    for h in (0, 1):
        ts2(("LU", 2 * h, 2 * h + 2), ("C2", 0, 2), ("RQ", h, h + 1), ("SH", h, h + 1), A.add, A.add)
    vput(("SI", 0, 256), ("LK", 0, 2), ("JS", 0, 32))
    vput(("INV", 0, 512), ("LU", 0, 4), ("JC", 0, 64))
    turn(("SR", 0, 128), ("SI", best // 2, best // 2 + 128))
    a, z = (0, 128) if high else (128, 0)
    turn(("TR", 0, 256), ("INV", best, best + 256))
    tt(("SU1", 0, 4), ("SR", 0, 128, 32), ("SR", 16, 128, 32), A.add)
    tt(("T1", 0, 8), ("TR", 0, 256, 32), ("TR", 16, 256, 32), A.add)
    tt(quad("SU2", 0, 4, 0, 64), quad("SU1", 0, 4, 0, 64), quad("SU1", 0, 4, 64, 64), A.add)
    tt(quad("T2", 0, 8, 0, 64), quad("T1", 0, 8, 0, 64), quad("T1", 0, 8, 64, 64), A.add)
    for name, src, n, p in (("ST", "SU2", 4, 0), ("ST", "SU2", 4, 32), ("T3", "T2", 8, 0), ("T3", "T2", 8, 32),
                            ("ST", "SU2", 4, 64), ("ST", "SU2", 4, 96)):
        tt(quad(name, 0, n, p), quad(src, 0, n, 0), quad(src, 0, n, 32), A.add)
    for p in (0, 64):
        copy(quad("NN", 0, 8, p, 64), quad("T3", 0, 8, 0, 64))
    scopy(("E1", 0, 256), ("UT", 256, 512))
    b = 128 if upper else 0
    scopy(("COLR", b, b + ZC), ("UT", 256, 256 + ZC))
    act(("VAL", 0, 32), ("JC", 0, 32), F.Identity, -128.0 if upper else float(ZC))
    for n in (32, 64):
        scopy(("HB", n, 2 * n), ("HB", 0, n))
    own, got = window("W1", a, a + 128), window("W1", z, z + 128)
    NEAR, MID = 192, 320
    cut = 64 * (3 - r4 if far else r4)
    pick_columns(window("Z", 128, 128 + ZC), window("X", 0, 256 + ZC), ("ZOFF", 0, 1))
    spick(("EX0", 0, NEAR), ("SCR", 0, 6), ("GOFF", 0, NEAR // 16))
    pick_columns(own, window("X", 0, 256), ("NN", 0, 8))
    split = 64 if cut == 64 else 128
    for b, e in ((0, split), (split, NEAR)):
        turn(("EX", b, e), ("EX0", b, e))

    mate = rank ^ 1
    exchange(mate, own, own, "arr1")
    arrive(got, "arr1")
    iota(("J256", 0, 256), [[N, 256]], N, 0)
    if r4 < 3:
        iota(("RK", 0, 3 - r4), [[1, 3 - r4]], rank + 1, 0)
    if r4:
        iota(("RK", 3 - r4, 3), [[1, r4]], far, 0)
    for o in range(O):
        hold("y", [("XT", 0, 512)], [])
        load("y", ("WT", 512 * o, 512 * o + 512), T.w[:, 512 * o:512 * o + 512], "dw%d" % o)
    spick(("EX0", NEAR, MID), ("SCR", 0, 10), ("GOFF", NEAR // 16, MID // 16))
    ops = (A.is_gt, A.is_ge) if far else (A.is_ge, A.is_gt)

    def beats(c, b, e, shift=0):
        s, o = ("ST", c, c + 1), OTH * c + shift
        if b < cut:
            ts(("CM", o + b, o + min(e, cut)), ("EX", b, min(e, cut)), s, ops[0])
        if max(b, cut) < e:
            ts(("CM", o + max(b, cut), o + e), ("EX", max(b, cut), e), s, ops[1])

    def count(c, n, init=0.0):
        m, end, o = n // 2, 224 * c + 224, OTH * c
        scan(("CS", end - m, end), ("CM", o, o + m), ("CM", o + m, o + n), init, A.add, A.add)

    way = 1.0 if far else -1.0

    def signs(b, e, shift=0):
        act(("TS", b + shift, e + shift), ("EX", b, e), F.Sign, ("ST", 3, 4), -1.0)

    signs(0, NEAR)
    spick(("EX0", MID, OTH), ("SCR", 0, 14), ("GOFF", MID // 16, OTH // 16))
    if cut:
        act(("TS", 0, cut), ("TS", 0, cut), F.Sign, way, 1.0, ("TS", MID, MID + 1))
    beats(0, 0, split)
    beats(0, split, NEAR)
    beats(1, 0, NEAR)
    turn(("EX", NEAR, MID), ("EX0", NEAR, MID))
    signs(NEAR, MID)
    spick(("SW", 0, 128), ("SF", 0, 256), ("NN", 0, 8))
    rest = ("TS", cut, MID + 1 if cut else MID)
    act(rest, rest, F.Relu, 0.0, way, ("PG", 1, 2))
    beats(2, 0, NEAR)
    for c in (0, 1):
        beats(c, NEAR, MID)
    turn(("EX", MID, OTH), ("EX0", MID, OTH))
    signs(MID, OTH, 1)
    rest = ("TS", MID + 1, OTH + 1)
    act(rest, rest, F.Relu, 0.0, way, ("PG", 0, 1))
    act(("PLR", 0, 1), ("C2P", 0, 1), F.Identity, 2 * ROUND - 7.5)
    act(("BASE", 0, 128), ("J256", 0, 128), F.Identity, 1.0, 1.0 / (128.0 * N))
    b = 0 if upper else ZC
    spick(("COLR", b, b + 128), ("J256", 0, 256), ("NN", 0, 8))
    beats(2, NEAR, MID)
    for c in range(3):
        beats(c, MID, OTH)
    for c in range(3):
        count(c, OTH)
    op = A.subtract if far else A.add
    ts2(quad("PA", 0, 1, 0, 64), quad("K0", 0, 1, 0, 64), quad("PG", 1, 2, 0, 64), quad("PG", 1, 2, 64, 64), op, op)
    mm(("BB", 0, 128), *U, *got)
    tt(quad("P2", 0, 3, 0, 64), quad("CS", 223, 672, 0, 64, 224), quad("CS", 223, 672, 64, 64, 224), A.add)
    ts2(quad("P2", 3, 4, 0, 64), quad("PA", 0, 1, 0, 64), quad("PG", 0, 1, 0, 64), quad("PG", 0, 1, 64, 64), op, op)
    for c in range(4):
        ts2(quad("P3", 0, 1, 32 * c), quad("P2", c, c + 1, 0), quad("P2", c, c + 1, 32), 128.0, A.add, A.min)
    tt(("G", 0, 128), ("BB", 0, 128), ("SW", 0, 128), A.is_lt if high else A.is_gt)
    ts(("RR", 0, 1), ("P3", 0, 1), ("PLR", 0, 1), A.add)
    scan(("FX", 0, 128), ("BASE", 0, 128), ("G", 0, 128), 0.0, A.max, A.subtract)
    ts2(("LUG", 0, 2), ("C2P", 0, 2), ("RR", 0, 1), ("P3", 0, 1), A.add, A.add)
    hold16(("FH", 0, 128), ("FX", 0, 128))
    vput(("E1", 0, 512), ("LUG", 0, 2), ("VAL", 0, 32))
    take16(("LOF", 0, 8), ("FH", 0, 128), 1.0, "SCB")
    turn(("TE", 0, 256), ("E1", 0, 256))
    z2 = 0 if upper else 128 + ZC
    S2 = window("Z", z2, z2 + 128)
    L2 = window("Z", 128 + ZC - z2, 256 + ZC - z2)
    pick_columns(S2, window("W1", 0, 256), ("LOF", 0, 8))
    send(rank ^ 2, S2[0], S2[0], "arr2", codes=True)
    arrive([L2[0]], "arr2")
    tt(("U1", 0, 8), ("TE", 0, 256, 32), ("TE", 16, 256, 32), A.add)
    fill(("IDB", 0, 32), 0.0)
    tt(quad("U2", 0, 8, 0, 64), quad("U1", 0, 8, 0, 64), quad("U1", 0, 8, 64, 64), A.add)
    mine = ("LV4", 8 * r4, 8 * r4 + 8)
    for p in (0, 32, 64, 96):
        tt(quad(*mine, p), quad("U2", 0, 8, 0), quad("U2", 0, 8, 32), A.add)
    spread(near, [mine] * 3, mine, "num1")
    arrive([("LV4", 8 * (m & 3), 8 * (m & 3) + 8) for m in near], "num1")
    send(rank ^ 2, S2[1], S2[1], "ars2")
    arrive([L2[1]], "ars2")
    ts(("LE", 0, 8), mine, 128.0 if upper else 0.0, A.add)
    vpick(("E2", 0, 128), ("COLR", 0, 128 + ZC), ("LE", 0, 8))
    for a in range(4):
        turn(quad("DT", 0, 32, 32 * a), quad("E2", 32 * a, 32 * a + 32, 32 * a))
    spread(near, [("IDN", i, i + 1) for i in [(rank - m - 1) % 4 for m in near]], ("DT", 0, 1), "num2")
    arrive([("IDN", 0, 3)], "num2")
    ts(("IDM", 0, 1), ("DT", 0, 1), float(rank), A.min)
    tt(("DD", 0, 16), ("LV4", 0, 16), ("LV4", 16, 32), A.add)
    quant(*window("W", 0, 128), ("WT", 0, 512))
    tt(("MM", 0, 8), ("DD", 0, 8), ("DD", 8, 16), A.add)
    quant(*window("W", 128, 256), ("WT", 512, 1024))
    ts(("LC", 0, 8), ("MM", 0, 8), 128.0, A.add)
    V4, L4 = window("V4", 0, 128), window("L4", 0, 128)
    pick_columns(V4, window("Z", 0, 256 + ZC), ("LC", 0, 8))
    mate = rank ^ 4
    exchange(mate, L4, V4, "arr3")
    arrive(L4, "arr3")
    got3 = ("IDN", 0, 3)
    tt(("IDR", 0, 3), got3, ("RK", 0, 3), A.min)
    scan(("IDC", 0, 3), got3, got3, ("DT", 0, 1), A.max, A.max)
    scan(("IDO", 0, 3), ("IDR", 0, 3), ("IDR", 0, 3), ("IDM", 0, 1), A.max, A.max)
    ts2(("IDO", 3, 4), ("IDC", 2, 3), 1.0 / N, 0.5, A.mult, A.subtract)
    send(mate, ("IDA", 0, 2), ("IDO", 2, 4), "num3")
    arrive([("IDA", 0, 2)], "num3")
    for o in range(O):
        mm(("BY%d" % o, 0, 128), *window("W", 128 * o, 128 * o + 128), *V4, True, False)
    for o in (1, 0):
        mm(("BY%d" % o, 0, 128), *window("W", 128 * o, 128 * o + 128), *L4, False, True)
    scopy(("YB", 128, 256), ("BY1", 0, 128))
    copy(("YB", 0, 128), ("BY0", 0, 128))
    do("y", lambda: g.sync.dma_start(T.y[:, :], ap(("YB", 0, 256))), [], [("YB", 0, 256)], "dy", 16)
    tt(("IDB", 0, 2), ("IDO", 2, 4), ("IDA", 0, 2), A.add)
    turn(("IDT", 0, 32), ("IDB", 0, 32))
    for row in (0, 1):
        do("s", lambda: g.scalar.dma_start(T.id[row, :], T.IDT[row:128:32, 0:32]), [], [("IDT", 0, 32)], "did", 16)
    late = ("t", "v", "s", "did", "dy")
    for sem in sorted(x for x in total if x not in late) + list(late):
        if known["g"].get(sem, 0) < total[sem]:
            g.wait_ge(T.sem[sem], total[sem])
